import numpy as np
import ml_dtypes


def mxq(x, axis, fmt="e4m3"):
    dtype, down = {"e4m3": (ml_dtypes.float8_e4m3fn, 7), "e5m2": (ml_dtypes.float8_e5m2, 14)}[fmt]
    v = np.moveaxis(np.asarray(x, np.float32).astype(ml_dtypes.bfloat16).astype(np.float64), axis, -1)
    blocks = v.reshape(v.shape[:-1] + (-1, 32))
    amax = np.abs(blocks).max(-1, keepdims=True)
    byte = np.maximum(np.where(amax > 0, np.frexp(amax)[1] - 1 + 127, 0) - down, 1)
    scale = np.exp2(byte - 127.0)
    codes = (blocks / scale).astype(np.float32).astype(dtype).astype(np.float64)
    return np.moveaxis((codes * scale).reshape(v.shape), -1, axis)


WIDE = False


def mx_kscale(k):
    if not WIDE:
        return np.ones(k)
    levels = np.array([10, -10, 5, -5, 0])
    if k % 512:
        return np.exp2(np.random.permutation(np.resize(levels, k // 32))).repeat(32)
    a = np.empty((k // 512, 16))
    for p in range(k // 512):
        a[p, :8] = np.random.permutation(np.resize(levels, 8))
        for g in range(8):
            far = levels[np.abs(levels - a[p, g]) >= 10]
            a[p, g + 8] = far[np.random.randint(len(far))]
    return np.exp2(a.ravel()).repeat(32)


BF16 = ml_dtypes.bfloat16


def bf(x):
    return np.asarray(x, np.float32).astype(BF16)


def f64(x):
    return np.asarray(x).astype(np.float64)

def planes(Y):
    n, m = Y.shape
    b = f64(bf(Y)).reshape(n // 32, 32, m)
    amax = np.abs(b).max(1)
    byte = np.clip(np.where(amax > 0, np.frexp(amax)[1] - 1 + 127 - 7, 1), 1, 254)
    codes = (b * np.exp2(127.0 - byte)[:, None, :]).reshape(n, m).astype(np.float32).astype(ml_dtypes.float8_e4m3fn).view(np.uint8)
    words = codes.reshape(n // 512, 128, 4, m).transpose(0, 1, 3, 2)
    return np.ascontiguousarray(words), np.ascontiguousarray(byte.astype(np.uint8).reshape(n // 512, 16, m))


B, S, D = 4, 512, 1024


def setup_inputs():
    s = mx_kscale(D)
    t = mx_kscale(S)
    r = np.exp(0.8 * np.random.randn(D))
    return {
        "latent": bf(np.random.randn(B, S, D) * s),
        "dyn_w": bf(np.random.randn(D, D) / np.sqrt(D) / s[:, None]),
        "slot_scale": bf((1 + 0.3 * np.random.randn(S)) * t),
        "next_w": bf(1.5 * np.random.randn(S, S) / np.sqrt(S) / t),
        "step": bf(r * (1 + 0.1 * np.random.randn(D))),
        "keep": bf(r * (1 + 0.1 * np.random.randn(D)) / s),
    }


def reference(latent, dyn_w, slot_scale, next_w, step, keep):
    z, w, c = f64(latent), f64(dyn_w), f64(slot_scale)
    v, st, ke = f64(next_w), f64(step), f64(keep)
    h = mxq(z, 2, "e4m3") @ mxq(w, 0, "e4m3")
    a = h / (1 + np.exp(-h)) * c[:, None]
    u = mxq(v, 1, "e4m3") @ mxq(a, 1, "e4m3")
    y = st * u + ke * z
    Y = y.reshape(B * S, D).T
    words, scales = planes(Y)
    return y, words, scales

@@ -1,0 +1,356 @@
+from contextlib import ExitStack
+
+import concourse.mybir as mybir
+from concourse.masks import make_identity
+
+B, S, D = 4, 512, 1024
+FLOPS = 2 * B * S * D * D + 2 * B * S * S * D
+
+F32 = mybir.dt.float32
+BF16 = mybir.dt.bfloat16
+I32 = mybir.dt.int32
+U32 = mybir.dt.uint32
+U8 = mybir.dt.uint8
+FP8X4 = mybir.dt.float8_e4m3fn_x4
+ACT = mybir.ActivationFunctionType
+ALU = mybir.AluOpType
+
+P = 128
+PACK = 4
+GROUP = P * PACK
+GROUPS = D // GROUP
+HALF = S // 2
+STEPS = B * GROUPS * PACK
+
+
+def tile_slot_mixing_latent_dynamics_h3_kernel(
+    tc, latent, dyn_w, slot_scale, next_w, step, keep, out_0, out_1, out_2
+):
+    nc = tc.nc
+    with ExitStack() as ctx:
+        const = ctx.enter_context(tc.tile_pool(name="const", bufs=1))
+        work = ctx.enter_context(tc.tile_pool(name="work", bufs=2))
+        psum = ctx.enter_context(tc.psum_pool(name="psum", bufs=2))
+        ctx.enter_context(tc.manual_schedule())
+
+        z_rows = {}
+        w_rows = {}
+
+        def load_z(b, hf):
+            rows = const.tile([P, 2, D], BF16, name="z_%d_%d" % (b, hf))
+            src = latent[b, hf * HALF : (hf + 1) * HALF, :]
+            nc.sync.dma_start(out=rows[:], in_=src.rearrange("(tb p) d -> p tb d", p=P))
+            z_rows[b, hf] = rows
+
+        def load_w(g, h):
+            rows = const.tile([P, PACK, GROUP], BF16, name="w_%d_%d" % (g, h))
+            src = dyn_w[g * GROUP : (g + 1) * GROUP, h * GROUP : (h + 1) * GROUP]
+            nc.sync.dma_start(out=rows[:], in_=src.rearrange("(p j) f -> p j f", j=PACK))
+            w_rows[g, h] = rows
+
+        keep_bf = const.tile([P, GROUPS, PACK], BF16)
+        step_bf = const.tile([P, GROUPS, PACK], BF16)
+        scale_bf = const.tile([P, PACK], BF16)
+        v_rows = const.tile([P, PACK, S], BF16)
+        load_w(0, 0)
+        nc.scalar.dma_start(out=keep_bf[:], in_=keep.rearrange("(g p t) -> p g t", p=P, t=PACK))
+        nc.scalar.dma_start(out=scale_bf[:], in_=slot_scale.rearrange("(p s) -> p s", s=PACK))
+        load_z(0, 0)
+        load_w(1, 0)
+        load_z(0, 1)
+        nc.sync.dma_start(out=v_rows[:], in_=next_w.rearrange("(jb p) i -> p jb i", p=P))
+        load_w(0, 1)
+        load_w(1, 1)
+        nc.sync.dma_start(out=step_bf[:], in_=step.rearrange("(g p t) -> p g t", p=P, t=PACK))
+        for b in range(1, B):
+            load_z(b, 0)
+            load_z(b, 1)
+
+        ident = const.tile([P, P], F32)
+        make_identity(nc, ident[:])
+        warm = const.tile([P, 1], F32)
+        nc.scalar.activation(out=warm[:], in_=ident[:, 0:1], func=ACT.Silu)
+        keep_f = const.tile([P, GROUPS, PACK], F32)
+        nc.scalar.copy(out=keep_f[:], in_=keep_bf[:])
+        scale_rep = const.tile([P, P, PACK], F32)
+        nc.scalar.copy(out=scale_rep[:], in_=scale_bf[:].unsqueeze(1).to_broadcast([P, P, PACK]))
+
+        y_scales = const.tile([P, GROUPS, B * S], U8, align_bytes=64)
+
+        def quantise(src, codes, scales):
+            nc.vector.quantize_mx(out=codes.bitcast(FP8X4), scales=scales, in_=src)
+
+        w_in = {}
+        w_mx = {}
+
+        def interleave_w(g, h):
+            grouped = work.tile([P, GROUP * PACK], BF16, tag="w_in", name="w_in", align_bytes=64)
+            nc.vector.tensor_copy(
+                out=grouped[:].rearrange("p (t m j) -> p t m j", t=PACK, j=PACK),
+                in_=w_rows[g, h][:].rearrange("p j (m t) -> p t m j", t=PACK),
+            )
+            w_in[g, h] = grouped
+
+        def quantise_w(g, h):
+            codes = const.tile([P, GROUP], U32, name="wc_%d_%d" % (g, h), align_bytes=64)
+            scales = const.tile([P, GROUP], U8, name="ws_%d_%d" % (g, h), align_bytes=64)
+            quantise(w_in[g, h][:], codes[:], scales[:])
+            w_mx[g, h] = (codes, scales)
+
+        def turn_words(rows, first_block, g, tag):
+            bank = psum.tile([P, 2, HALF], F32, tag=tag, name="turned")
+            words = rows[:].bitcast(F32)
+            for tb in range(2):
+                for u in range(2):
+                    nc.tensor.transpose(
+                        bank[:, u, tb * P : (tb + 1) * P],
+                        words[:, first_block + tb, 256 * g + u : 256 * (g + 1) : 2],
+                        ident[:],
+                    )
+            return bank
+
+        z_bank = {}
+        z_in = {}
+        z_mx = {}
+        kept = {}
+
+        def turn_z(b, g, hf, tag="zt"):
+            z_bank[b, g, hf] = turn_words(z_rows[b, hf], 0, g, tag)
+
+        def copy_z(b, g, hf):
+            if hf == 0:
+                z_in[b, g] = work.tile([P, S * 2], F32, tag="z_in", name="z_in", bufs=3, align_bytes=64)
+            dst = z_in[b, g][:].rearrange("p (s m u) -> p s m u", s=PACK, u=2)
+            nc.scalar.copy(
+                out=dst[:, :, 64 * hf : 64 * (hf + 1), :],
+                in_=z_bank[b, g, hf][:].rearrange("p u (m s) -> p s m u", s=PACK),
+            )
+
+        def scale_z(b, g, hf, slots):
+            if (b, g) not in kept:
+                kept[b, g] = work.tile([P, PACK, S], F32, tag="kept", name="kept", bufs=5)
+            halves = z_bank[b, g, hf][:].bitcast(BF16)
+            for t in slots:
+                nc.scalar.activation(
+                    out=kept[b, g][:, t, hf * HALF : (hf + 1) * HALF],
+                    in_=halves[:, t // 2, t % 2 : 2 * HALF : 2],
+                    func=ACT.Copy,
+                    scale=keep_f[:, g, t : t + 1],
+                )
+
+        def quantise_z(b, g):
+            codes = work.tile([P, S], U32, tag="zc", name="zc", bufs=4, align_bytes=64)
+            scales = work.tile([P, S], U8, tag="zs", name="zs", bufs=4, align_bytes=64)
+            quantise(z_in[b, g][:].bitcast(BF16), codes[:], scales[:])
+            z_mx[b, g] = (codes, scales)
+
+        v_in = const.tile([P, S * 2], F32, align_bytes=64)
+        v_codes = const.tile([P, S], U32, align_bytes=64)
+        v_scales = const.tile([P, S], U8, align_bytes=64)
+        v_bank = {}
+
+        def turn_v(hf):
+            v_bank[hf] = turn_words(v_rows, 2 * hf, 0, "s2")
+
+        def copy_v(hf):
+            dst = v_in[:].rearrange("p (j u) -> p j u", u=2)
+            nc.scalar.copy(
+                out=dst[:, hf * HALF : (hf + 1) * HALF, :],
+                in_=v_bank[hf][:].rearrange("p u j -> p j u"),
+            )
+
+        h_bank = {}
+        silu = {}
+        a_in = {}
+        a_mx = {}
+        u_bank = {}
+        y_turned = {}
+        y_bank = {}
+        y_rows = {}
+        y_in = {}
+
+        def where(i):
+            return i // (GROUPS * PACK), (i // PACK) % GROUPS, i % PACK
+
+        def stage_one(i):
+            b, h, t = where(i)
+            bank = psum.tile([P, PACK, P], F32, tag="s1", name="h_bank")
+            cols = slice(t * P, (t + 1) * P)
+            for s in range(PACK):
+                slots = slice(s * P, (s + 1) * P)
+                for g in range(GROUPS):
+                    nc.tensor.matmul_mx(
+                        out=bank[:, s, :],
+                        lhsT=z_mx[b, g][0][:, slots].bitcast(FP8X4),
+                        lhsT_scale=z_mx[b, g][1][:, slots],
+                        rhs=w_mx[g, h][0][:, cols].bitcast(FP8X4),
+                        rhs_scale=w_mx[g, h][1][:, cols],
+                        start=(g == 0),
+                        stop=(g == GROUPS - 1),
+                    )
+            h_bank[i] = bank
+
+        def activate(i):
+            silu[i] = work.tile([P, P * PACK], F32, tag="silu", name="silu", bufs=3)
+            nc.scalar.activation(
+                out=silu[i][:].rearrange("p (m s) -> p m s", s=PACK),
+                in_=h_bank[i][:].rearrange("p s m -> p m s"),
+                func=ACT.Silu,
+            )
+
+        def scale_a(i):
+            a_in[i] = work.tile([P, P * PACK], BF16, tag="a_in", name="a_in", bufs=3, align_bytes=64)
+            nc.vector.tensor_tensor(
+                out=a_in[i][:],
+                in0=silu[i][:],
+                in1=scale_rep[:].rearrange("p m s -> p (m s)"),
+                op=ALU.mult,
+            )
+
+        def quantise_a(i):
+            codes = work.tile([P, P], U32, tag="ac", name="ac", bufs=3, align_bytes=64)
+            scales = work.tile([P, P], U8, tag="as", name="as", bufs=3, align_bytes=64)
+            quantise(a_in[i][:], codes[:], scales[:])
+            a_mx[i] = (codes, scales)
+
+        def stage_two(i):
+            bank = psum.tile([P, S], F32, tag="s2", name="u_bank")
+            nc.tensor.matmul_mx(
+                out=bank[:],
+                lhsT=a_mx[i][0][:].bitcast(FP8X4),
+                lhsT_scale=a_mx[i][1][:],
+                rhs=v_codes[:].bitcast(FP8X4),
+                rhs_scale=v_scales[:],
+                start=True,
+                stop=True,
+            )
+            u_bank[i] = bank
+
+        def residual(i):
+            b, g, t = where(i)
+            if t == 0:
+                y_turned[b, g] = work.tile([P, PACK, S], F32, tag="yt", name="y_turned", bufs=3)
+            nc.vector.scalar_tensor_tensor(
+                out=y_turned[b, g][:, t, :],
+                in0=u_bank[i][:],
+                scalar=step_bf[:, g, t : t + 1],
+                in1=kept[b, g][:, t, :],
+                op0=ALU.mult,
+                op1=ALU.add,
+            )
+
+        def turn_y(i):
+            b, g, jb = where(i)
+            bank = psum.tile([P, PACK, P], F32, tag="yt", name="y_bank")
+            for t in range(PACK):
+                nc.tensor.transpose(bank[:, t, :], y_turned[b, g][:, t, jb * P : (jb + 1) * P], ident[:])
+            y_bank[i] = bank
+
+        def store_y(i):
+            b, g, jb = where(i)
+            if jb % 2 == 0:
+                y_rows[i // 2] = work.tile([P, 2, GROUP], F32, tag="y_rows", name="y_rows", bufs=4)
+            rows = y_rows[i // 2]
+            nc.scalar.copy(
+                out=rows[:, jb % 2, :].rearrange("p (m t) -> p m t", t=PACK),
+                in_=y_bank[i][:].rearrange("p t m -> p m t"),
+            )
+            if jb % 2 == 1:
+                dst = out_0[b, (jb - 1) * P : (jb + 1) * P, g * GROUP : (g + 1) * GROUP]
+                nc.sync.dma_start(out=dst.rearrange("(jb p) f -> p jb f", p=P), in_=rows[:])
+
+        def round_y(b, g, hf):
+            if hf == 0:
+                y_in[b, g] = work.tile([P, S, PACK], BF16, tag="y_in", name="y_in", align_bytes=64)
+            cols = slice(hf * HALF, (hf + 1) * HALF)
+            nc.vector.tensor_copy(
+                out=y_in[b, g][:, cols, :].rearrange("p (c i) t -> p c t i", i=4),
+                in_=y_turned[b, g][:, :, cols].rearrange("p t (c i) -> p c t i", i=4),
+            )
+
+        def quantise_y(b, g):
+            codes = work.tile([P, S], U32, tag="yc", name="yc", bufs=3, align_bytes=64)
+            quantise(y_in[b, g][:].rearrange("p j t -> p (j t)"), codes[:], y_scales[:, g, b * S : (b + 1) * S])
+            dst = out_1[g, :, b * S : (b + 1) * S, :].rearrange("p m t -> p (m t)")
+            nc.sync.dma_start(out=dst.bitcast(I32), in_=codes[:].bitcast(I32))
+
+        turn_z(0, 0, 0)
+        turn_z(0, 1, 0)
+        turn_z(0, 0, 1, "yt")
+        turn_z(0, 1, 1, "yt")
+        turn_v(0)
+        turn_v(1)
+        interleave_w(0, 0)
+        copy_z(0, 0, 0)
+        copy_z(0, 1, 0)
+        scale_z(0, 0, 0, range(PACK))
+        interleave_w(1, 0)
+        quantise_w(0, 0)
+        copy_z(0, 0, 1)
+        copy_z(0, 1, 1)
+        quantise_w(1, 0)
+        quantise_z(0, 0)
+        quantise_z(0, 1)
+        copy_v(0)
+        copy_v(1)
+        scale_z(0, 1, 0, range(PACK))
+        turn_z(1, 0, 0)
+
+        def z_place(j):
+            q = (j + 2) // 2
+            return 1 + q // 4, (q // 2) % 2, q % 2
+
+        last = STEPS + 8
+        for j in range(last + 1):
+            if j < STEPS:
+                stage_one(j)
+            if 0 <= j - 3 < STEPS:
+                stage_two(j - 3)
+            if 0 <= j - 8 < STEPS:
+                turn_y(j - 8)
+            if j % 2 == 0 and z_place(j)[0] < B:
+                turn_z(*z_place(j))
+            if 0 <= j - 1 < STEPS:
+                activate(j - 1)
+            if 0 <= j - 9 < STEPS:
+                store_y(j - 9)
+            if j == 0:
+                copy_z(1, 0, 0)
+                scale_z(0, 0, 1, range(PACK))
+                scale_z(1, 0, 0, range(PACK))
+            elif j % 2 == 1 and z_place(j - 1)[0] < B:
+                copy_z(*z_place(j - 1))
+                scale_z(*z_place(j - 1), range(0, 1))
+            elif j % 2 == 0 and z_place(j - 2)[0] < B:
+                scale_z(*z_place(j - 2), range(1, PACK))
+            if j == 3:
+                scale_z(0, 1, 1, range(PACK))
+            if j == 0:
+                interleave_w(0, 1)
+                quantise(v_in[:].bitcast(BF16), v_codes[:], v_scales[:])
+            if j == 1:
+                interleave_w(1, 1)
+                quantise_w(0, 1)
+            if 0 <= j - 2 < STEPS:
+                scale_a(j - 2)
+            if j == 2:
+                quantise_w(1, 1)
+            if 0 <= j - 4 < STEPS:
+                residual(j - 4)
+            if 0 <= j - 2 < STEPS:
+                quantise_a(j - 2)
+            if 0 <= j - 8 < STEPS:
+                b, g, k = where(j - 8)
+                if k < 2:
+                    round_y(b, g, k)
+                if k == 3:
+                    quantise_y(b, g)
+            if j % 4 == 2 and j // 8 + 1 < B:
+                quantise_z(j // 8 + 1, (j // 4) % 2)
+
+        scale_words = out_2.bitcast(I32)
+        for q in range(4):
+            nc.sync.dma_start(
+                out=scale_words[:, 4 * q : 4 * q + 4, :].rearrange("g r m -> r g m"),
+                in_=y_scales[32 * q : 32 * q + 4].bitcast(I32),
+            )

@@ -55,14 +55,16 @@ def tile_slot_mixing_latent_dynamics_h3_kernel(
         load_w(0, 0)
         nc.scalar.dma_start(out=keep_bf[:], in_=keep.rearrange("(g p t) -> p g t", p=P, t=PACK))
         nc.scalar.dma_start(out=scale_bf[:], in_=slot_scale.rearrange("(p s) -> p s", s=PACK))
-        load_z(0, 0)
         load_w(1, 0)
+        load_z(0, 0)
         load_z(0, 1)
         nc.sync.dma_start(out=v_rows[:], in_=next_w.rearrange("(jb p) i -> p jb i", p=P))
         load_w(0, 1)
         load_w(1, 1)
+        load_z(1, 0)
+        load_z(1, 1)
         nc.sync.dma_start(out=step_bf[:], in_=step.rearrange("(g p t) -> p g t", p=P, t=PACK))
-        for b in range(1, B):
+        for b in range(2, B):
             load_z(b, 0)
             load_z(b, 1)
 
@@ -71,31 +73,50 @@ def tile_slot_mixing_latent_dynamics_h3_kernel(
         warm = const.tile([P, 1], F32)
         nc.scalar.activation(out=warm[:], in_=ident[:, 0:1], func=ACT.Silu)
         keep_f = const.tile([P, GROUPS, PACK], F32)
-        nc.scalar.copy(out=keep_f[:], in_=keep_bf[:])
         scale_rep = const.tile([P, P, PACK], F32)
-        nc.scalar.copy(out=scale_rep[:], in_=scale_bf[:].unsqueeze(1).to_broadcast([P, P, PACK]))
 
         y_scales = const.tile([P, GROUPS, B * S], U8, align_bytes=64)
 
         def quantise(src, codes, scales):
             nc.vector.quantize_mx(out=codes.bitcast(FP8X4), scales=scales, in_=src)
 
+        warm_in = const.tile([P, S], BF16, align_bytes=64)
+        warm_codes = const.tile([P, P], U32, align_bytes=64)
+        warm_scales = const.tile([P, P], U8, align_bytes=64)
+        nc.vector.memset(warm_in[:], 1.0)
+        quantise(warm_in[:], warm_codes[:], warm_scales[:])
+
+        def warm_up(passes, warm_codes, warm_scales, tag="s1"):
+            bank = psum.tile([P, P], F32, tag=tag, name="warm_bank")
+            for n in range(passes):
+                nc.tensor.matmul_mx(
+                    out=bank[:],
+                    lhsT=warm_codes[:, 0:P].bitcast(FP8X4),
+                    lhsT_scale=warm_scales[:, 0:P],
+                    rhs=warm_codes[:].bitcast(FP8X4),
+                    rhs_scale=warm_scales[:],
+                    start=True,
+                    stop=True,
+                )
+
         w_in = {}
         w_mx = {}
 
-        def interleave_w(g, h):
-            grouped = work.tile([P, GROUP * PACK], BF16, tag="w_in", name="w_in", align_bytes=64)
-            nc.vector.tensor_copy(
-                out=grouped[:].rearrange("p (t m j) -> p t m j", t=PACK, j=PACK),
-                in_=w_rows[g, h][:].rearrange("p j (m t) -> p t m j", t=PACK),
-            )
-            w_in[g, h] = grouped
+        def interleave_w(g, i, engine):
+            h, t = i // PACK, i % PACK
+            grouped = work.tile([P, P, PACK], BF16, tag="w_in", name="w_in", bufs=8, align_bytes=64)
+            src = w_rows[g, h][:].rearrange("p j (m t) -> p t m j", t=PACK)[:, t, :, :]
+            if engine == "vector":
+                nc.vector.tensor_copy(out=grouped[:], in_=src)
+            else:
+                nc.scalar.copy(out=grouped[:], in_=src)
+            w_in[g, i] = grouped
 
-        def quantise_w(g, h):
-            codes = const.tile([P, GROUP], U32, name="wc_%d_%d" % (g, h), align_bytes=64)
-            scales = const.tile([P, GROUP], U8, name="ws_%d_%d" % (g, h), align_bytes=64)
-            quantise(w_in[g, h][:], codes[:], scales[:])
-            w_mx[g, h] = (codes, scales)
+        def quantise_w(g, i):
+            codes = const.tile([P, P], U32, name="wc_%d_%d" % (g, i), align_bytes=64)
+            scales = const.tile([P, P], U8, name="ws_%d_%d" % (g, i), align_bytes=64)
+            quantise(w_in[g, i][:].rearrange("p m j -> p (m j)"), codes[:], scales[:])
+            w_mx[g, i] = (codes, scales)
 
         def turn_words(rows, first_block, g, tag):
             bank = psum.tile([P, 2, HALF], F32, tag=tag, name="turned")
@@ -138,6 +159,17 @@ def tile_slot_mixing_latent_dynamics_h3_kernel(
                     scale=keep_f[:, g, t : t + 1],
                 )
 
+        def scale_z_vector(b, g, hf, u):
+            if (b, g) not in kept:
+                kept[b, g] = work.tile([P, PACK, S], F32, tag="kept", name="kept", bufs=5)
+            halves = z_bank[b, g, hf][:].bitcast(BF16)
+            nc.vector.tensor_tensor(
+                out=kept[b, g][:, 2 * u : 2 * u + 2, hf * HALF : (hf + 1) * HALF],
+                in0=halves[:, u, :].rearrange("p (j e) -> p e j", e=2),
+                in1=keep_f[:, g, 2 * u : 2 * u + 2].unsqueeze(2).to_broadcast([P, 2, HALF]),
+                op=ALU.mult,
+            )
+
         def quantise_z(b, g):
             codes = work.tile([P, S], U32, tag="zc", name="zc", bufs=4, align_bytes=64)
             scales = work.tile([P, S], U8, tag="zs", name="zs", bufs=4, align_bytes=64)
@@ -175,7 +207,6 @@ def tile_slot_mixing_latent_dynamics_h3_kernel(
         def stage_one(i):
             b, h, t = where(i)
             bank = psum.tile([P, PACK, P], F32, tag="s1", name="h_bank")
-            cols = slice(t * P, (t + 1) * P)
             for s in range(PACK):
                 slots = slice(s * P, (s + 1) * P)
                 for g in range(GROUPS):
@@ -183,8 +214,8 @@ def tile_slot_mixing_latent_dynamics_h3_kernel(
                         out=bank[:, s, :],
                         lhsT=z_mx[b, g][0][:, slots].bitcast(FP8X4),
                         lhsT_scale=z_mx[b, g][1][:, slots],
-                        rhs=w_mx[g, h][0][:, cols].bitcast(FP8X4),
-                        rhs_scale=w_mx[g, h][1][:, cols],
+                        rhs=w_mx[g, h * PACK + t][0][:].bitcast(FP8X4),
+                        rhs_scale=w_mx[g, h * PACK + t][1][:],
                         start=(g == 0),
                         stop=(g == GROUPS - 1),
                     )
@@ -239,118 +270,181 @@ def tile_slot_mixing_latent_dynamics_h3_kernel(
                 op1=ALU.add,
             )
 
-        def turn_y(i):
+        def turn_y(i, slots, tag="yt"):
             b, g, jb = where(i)
-            bank = psum.tile([P, PACK, P], F32, tag="yt", name="y_bank")
-            for t in range(PACK):
-                nc.tensor.transpose(bank[:, t, :], y_turned[b, g][:, t, jb * P : (jb + 1) * P], ident[:])
-            y_bank[i] = bank
+            if i not in y_bank:
+                y_bank[i] = psum.tile([P, PACK, P], F32, tag=tag, name="y_bank")
+            for t in slots:
+                nc.tensor.transpose(y_bank[i][:, t, :], y_turned[b, g][:, t, jb * P : (jb + 1) * P], ident[:])
 
-        def store_y(i):
+        def store_y(i, engine, group):
             b, g, jb = where(i)
-            if jb % 2 == 0:
-                y_rows[i // 2] = work.tile([P, 2, GROUP], F32, tag="y_rows", name="y_rows", bufs=4)
-            rows = y_rows[i // 2]
-            nc.scalar.copy(
-                out=rows[:, jb % 2, :].rearrange("p (m t) -> p m t", t=PACK),
-                in_=y_bank[i][:].rearrange("p t m -> p m t"),
-            )
-            if jb % 2 == 1:
-                dst = out_0[b, (jb - 1) * P : (jb + 1) * P, g * GROUP : (g + 1) * GROUP]
-                nc.sync.dma_start(out=dst.rearrange("(jb p) f -> p jb f", p=P), in_=rows[:])
+            if jb % group == 0:
+                y_rows[b, g] = work.tile([P, group, GROUP], F32, tag="y_rows", name="y_rows", bufs=4)
+            rows = y_rows[b, g]
+            dst = rows[:, jb % group, :].rearrange("p (m t) -> p m t", t=PACK)
+            src = y_bank[i][:].rearrange("p t m -> p m t")
+            if engine == "vector":
+                nc.vector.tensor_copy(out=dst, in_=src)
+            else:
+                nc.scalar.copy(out=dst, in_=src)
+            if jb % group == group - 1:
+                hbm = out_0[b, (jb + 1 - group) * P : (jb + 1) * P, g * GROUP : (g + 1) * GROUP]
+                nc.sync.dma_start(out=hbm.rearrange("(jb p) f -> p jb f", p=P), in_=rows[:])
 
-        def round_y(b, g, hf):
-            if hf == 0:
+        def store_scales(first, count):
+            cols = slice(first * S // 4, (first + count) * S // 4)
+            for q in range(4):
+                nc.sync.dma_start(
+                    out=out_2.bitcast(I32)[:, 4 * q : 4 * q + 4, cols].rearrange("g r m -> r g m"),
+                    in_=y_scales[32 * q : 32 * q + 4].bitcast(I32)[:, :, cols],
+                )
+
+        def round_y(b, g, first, count, engine):
+            if (b, g) not in y_in:
                 y_in[b, g] = work.tile([P, S, PACK], BF16, tag="y_in", name="y_in", align_bytes=64)
-            cols = slice(hf * HALF, (hf + 1) * HALF)
-            nc.vector.tensor_copy(
-                out=y_in[b, g][:, cols, :].rearrange("p (c i) t -> p c t i", i=4),
-                in_=y_turned[b, g][:, :, cols].rearrange("p t (c i) -> p c t i", i=4),
-            )
+            cols = slice(first * P, (first + count) * P)
+            dst = y_in[b, g][:, cols, :].rearrange("p (c i) t -> p c t i", i=4)
+            src = y_turned[b, g][:, :, cols].rearrange("p t (c i) -> p c t i", i=4)
+            if engine == "vector":
+                nc.vector.tensor_copy(out=dst, in_=src)
+            else:
+                nc.scalar.copy(out=dst, in_=src)
 
-        def quantise_y(b, g):
-            codes = work.tile([P, S], U32, tag="yc", name="yc", bufs=3, align_bytes=64)
-            quantise(y_in[b, g][:].rearrange("p j t -> p (j t)"), codes[:], y_scales[:, g, b * S : (b + 1) * S])
-            dst = out_1[g, :, b * S : (b + 1) * S, :].rearrange("p m t -> p (m t)")
+        def quantise_y(b, g, first=0, count=S):
+            codes = work.tile([P, count], U32, tag="yc", name="yc", bufs=3, align_bytes=64)
+            src = y_in[b, g][:, first : first + count, :].rearrange("p j t -> p (j t)")
+            cols = slice(b * S + first, b * S + first + count)
+            quantise(src, codes[:], y_scales[:, g, cols])
+            dst = out_1[g, :, cols, :].rearrange("p m t -> p (m t)")
             nc.sync.dma_start(out=dst.bitcast(I32), in_=codes[:].bitcast(I32))
 
+        warm_up(26, warm_codes, warm_scales)
+        interleave_w(0, 0, "vector")
+        interleave_w(0, 1, "vector")
+        quantise_w(0, 0)
+        warm_up(16, *w_mx[0, 0])
         turn_z(0, 0, 0)
-        turn_z(0, 1, 0)
-        turn_z(0, 0, 1, "yt")
+        turn_z(0, 1, 0, "yt")
+        turn_z(0, 0, 1)
         turn_z(0, 1, 1, "yt")
-        turn_v(0)
-        turn_v(1)
-        interleave_w(0, 0)
+        interleave_w(0, 2, "vector")
+        interleave_w(0, 3, "scalar")
+        nc.scalar.copy(out=keep_f[:], in_=keep_bf[:])
+        for t in range(PACK):
+            interleave_w(1, t, "vector" if t < 2 else "scalar")
+        nc.scalar.copy(out=scale_rep[:], in_=scale_bf[:].unsqueeze(1).to_broadcast([P, P, PACK]))
+        for g in range(GROUPS):
+            for t in range(PACK):
+                if (g, t) != (0, 0):
+                    quantise_w(g, t)
+        warm_up(8, *w_mx[1, 3])
         copy_z(0, 0, 0)
         copy_z(0, 1, 0)
-        scale_z(0, 0, 0, range(PACK))
-        interleave_w(1, 0)
-        quantise_w(0, 0)
+        scale_z_vector(0, 0, 0, 0)
         copy_z(0, 0, 1)
         copy_z(0, 1, 1)
-        quantise_w(1, 0)
+        scale_z_vector(0, 0, 0, 1)
         quantise_z(0, 0)
         quantise_z(0, 1)
-        copy_v(0)
-        copy_v(1)
-        scale_z(0, 1, 0, range(PACK))
-        turn_z(1, 0, 0)
 
         def z_place(j):
-            q = (j + 2) // 2
+            q = j - 2 if j < 6 else (j + 2) // 2
             return 1 + q // 4, (q // 2) % 2, q % 2
 
-        last = STEPS + 8
-        for j in range(last + 1):
+        def turns_z(j):
+            return 2 <= j < 6 or (j >= 6 and j % 2 == 0 and z_place(j)[0] < B)
+
+        tail = STEPS - 2 * PACK
+        for j in range(STEPS + 1):
             if j < STEPS:
                 stage_one(j)
+            if j == 0:
+                turn_v(0)
+                turn_v(1)
             if 0 <= j - 3 < STEPS:
                 stage_two(j - 3)
-            if 0 <= j - 8 < STEPS:
-                turn_y(j - 8)
-            if j % 2 == 0 and z_place(j)[0] < B:
+            if 0 <= j - 8 < tail:
+                turn_y(j - 8, range(PACK))
+            if turns_z(j):
                 turn_z(*z_place(j))
             if 0 <= j - 1 < STEPS:
                 activate(j - 1)
-            if 0 <= j - 9 < STEPS:
-                store_y(j - 9)
+            if 0 <= j - 9 < tail:
+                store_y(j - 9, "scalar", 2)
             if j == 0:
-                copy_z(1, 0, 0)
                 scale_z(0, 0, 1, range(PACK))
-                scale_z(1, 0, 0, range(PACK))
-            elif j % 2 == 1 and z_place(j - 1)[0] < B:
-                copy_z(*z_place(j - 1))
-                scale_z(*z_place(j - 1), range(0, 1))
-            elif j % 2 == 0 and z_place(j - 2)[0] < B:
-                scale_z(*z_place(j - 2), range(1, PACK))
-            if j == 3:
-                scale_z(0, 1, 1, range(PACK))
-            if j == 0:
-                interleave_w(0, 1)
-                quantise(v_in[:].bitcast(BF16), v_codes[:], v_scales[:])
             if j == 1:
-                interleave_w(1, 1)
-                quantise_w(0, 1)
+                copy_v(0)
+                copy_v(1)
+            if j == 2:
+                scale_z(0, 1, 1, range(2))
+            if turns_z(j - 1):
+                copy_z(*z_place(j - 1))
+                scale_z(*z_place(j - 1), range(PACK if j < 7 else 1))
+            elif j > 7 and turns_z(j - 2):
+                scale_z(*z_place(j - 2), range(1, PACK if j % 1000 != 0 else 2))
+            if 0 <= j - 8 < tail and j - 8 >= 20:
+                b, g, k = where(j - 8)
+                round_y(b, g, k, 1, "scalar")
+            pieces = [(0, PACK + 2 * j), (0, PACK + 2 * j + 1)] if j < 2 else [(1, j + 2)] if j < 6 else []
+            for g, i in pieces:
+                interleave_w(g, i, "vector")
             if 0 <= j - 2 < STEPS:
                 scale_a(j - 2)
             if j == 2:
-                quantise_w(1, 1)
+                quantise(v_in[:].bitcast(BF16), v_codes[:], v_scales[:])
             if 0 <= j - 4 < STEPS:
                 residual(j - 4)
+            for g, i in pieces:
+                quantise_w(g, i)
             if 0 <= j - 2 < STEPS:
                 quantise_a(j - 2)
-            if 0 <= j - 8 < STEPS:
+            if j in (3, 4):
+                scale_z_vector(0, 1, 0, j - 3)
+            if j == 5 and 2 == 2:
+                scale_z_vector(0, 1, 1, 1)
+            if j > 7 and j % 1000 == 0 and turns_z(j - 2):
+                scale_z_vector(*z_place(j - 2), 1)
+            if j >= 12 and j % 4 == 0:
+                b, g, k = where(j - 12)
+                quantise_y(b, g)
+                if g == 1:
+                    store_scales(b, 1)
+            if 0 <= j - 8 < min(tail, 20):
                 b, g, k = where(j - 8)
-                if k < 2:
-                    round_y(b, g, k)
-                if k == 3:
-                    quantise_y(b, g)
-            if j % 4 == 2 and j // 8 + 1 < B:
+                round_y(b, g, k, 1, "vector")
+            if j > 7 and j % 4 == 2 and j // 8 + 1 < B:
                 quantise_z(j // 8 + 1, (j // 4) % 2)
+            if j in (5, 6):
+                quantise_z(1, j - 5)
 
-        scale_words = out_2.bitcast(I32)
-        for q in range(4):
-            nc.sync.dma_start(
-                out=scale_words[:, 4 * q : 4 * q + 4, :].rearrange("g r m -> r g m"),
-                in_=y_scales[32 * q : 32 * q + 4].bitcast(I32),
-            )
+        tags = ("zt", "zt", "yt", "yt")
+        for jb in range(PACK):
+            turn_y(tail + jb, range(PACK), tags[jb])
+        stage_two(STEPS - 2)
+        warm_up(6, warm_codes, warm_scales)
+        scale_a(STEPS - 1)
+        residual(STEPS - 3)
+        quantise_a(STEPS - 1)
+        stage_two(STEPS - 1)
+        store_y(tail, "scalar", 2)
+        store_y(tail + 1, "scalar", 2)
+        round_y(B - 1, 0, 0, 1, "scalar")
+        store_y(tail + 2, "scalar", 2)
+        store_y(tail + 3, "scalar", 2)
+        residual(STEPS - 2)
+        round_y(B - 1, 0, 1, PACK - 1, "vector")
+        residual(STEPS - 1)
+        quantise_y(B - 1, 0)
+        for jb in range(PACK):
+            turn_y(tail + PACK + jb, range(PACK - 1), tags[jb])
+        for jb in range(PACK):
+            turn_y(tail + PACK + jb, range(PACK - 1, PACK), tags[jb])
+        round_y(B - 1, 1, 0, PACK, "vector")
+        store_y(tail + PACK, "scalar", 2)
+        store_y(tail + PACK + 1, "scalar", 2)
+        quantise_y(B - 1, 1)
+        store_y(tail + PACK + 2, "scalar", 2)
+        store_y(tail + PACK + 3, "scalar", 2)
+        store_scales(B - 1, 1)

@@ -58,11 +58,11 @@ def tile_slot_mixing_latent_dynamics_h3_kernel(
         load_w(1, 0)
         load_z(0, 0)
         load_z(0, 1)
-        nc.sync.dma_start(out=v_rows[:], in_=next_w.rearrange("(jb p) i -> p jb i", p=P))
         load_w(0, 1)
-        load_w(1, 1)
         load_z(1, 0)
         load_z(1, 1)
+        nc.sync.dma_start(out=v_rows[:], in_=next_w.rearrange("(jb p) i -> p jb i", p=P))
+        load_w(1, 1)
         nc.sync.dma_start(out=step_bf[:], in_=step.rearrange("(g p t) -> p g t", p=P, t=PACK))
         for b in range(2, B):
             load_z(b, 0)
@@ -138,11 +138,11 @@ def tile_slot_mixing_latent_dynamics_h3_kernel(
         def turn_z(b, g, hf, tag="zt"):
             z_bank[b, g, hf] = turn_words(z_rows[b, hf], 0, g, tag)
 
-        def copy_z(b, g, hf):
+        def copy_z(b, g, hf, engine="scalar"):
             if hf == 0:
                 z_in[b, g] = work.tile([P, S * 2], F32, tag="z_in", name="z_in", bufs=3, align_bytes=64)
             dst = z_in[b, g][:].rearrange("p (s m u) -> p s m u", s=PACK, u=2)
-            nc.scalar.copy(
+            (nc.scalar.copy if engine == "scalar" else nc.vector.tensor_copy)(
                 out=dst[:, :, 64 * hf : 64 * (hf + 1), :],
                 in_=z_bank[b, g, hf][:].rearrange("p u (m s) -> p s m u", s=PACK),
             )
@@ -244,8 +244,8 @@ def tile_slot_mixing_latent_dynamics_h3_kernel(
             quantise(a_in[i][:], codes[:], scales[:])
             a_mx[i] = (codes, scales)
 
-        def stage_two(i):
-            bank = psum.tile([P, S], F32, tag="s2", name="u_bank")
+        def stage_two(i, tag="s2"):
+            bank = psum.tile([P, S], F32, tag=tag, name="u_bank")
             nc.tensor.matmul_mx(
                 out=bank[:],
                 lhsT=a_mx[i][0][:].bitcast(FP8X4),
@@ -280,7 +280,7 @@ def tile_slot_mixing_latent_dynamics_h3_kernel(
         def store_y(i, engine, group):
             b, g, jb = where(i)
             if jb % group == 0:
-                y_rows[b, g] = work.tile([P, group, GROUP], F32, tag="y_rows", name="y_rows", bufs=4)
+                y_rows[b, g] = work.tile([P, group, GROUP], F32, tag="y_rows", name="y_rows", bufs=6)
             rows = y_rows[b, g]
             dst = rows[:, jb % group, :].rearrange("p (m t) -> p m t", t=PACK)
             src = y_bank[i][:].rearrange("p t m -> p m t")
@@ -300,24 +300,34 @@ def tile_slot_mixing_latent_dynamics_h3_kernel(
                     in_=y_scales[32 * q : 32 * q + 4].bitcast(I32)[:, :, cols],
                 )
 
-        def round_y(b, g, first, count, engine):
-            if (b, g) not in y_in:
-                y_in[b, g] = work.tile([P, S, PACK], BF16, tag="y_in", name="y_in", align_bytes=64)
-            cols = slice(first * P, (first + count) * P)
-            dst = y_in[b, g][:, cols, :].rearrange("p (c i) t -> p c t i", i=4)
-            src = y_turned[b, g][:, :, cols].rearrange("p t (c i) -> p c t i", i=4)
+        def round_y(b, g, hf, first, last, engine):
+            if (b, g, hf) not in y_in:
+                tag = "y_last" if (b, g, hf) > (B - 1, 0, 0) else "y_in"
+                y_in[b, g, hf] = work.tile([P, HALF, PACK], BF16, tag=tag, name=tag, bufs=1 if tag == "y_in" else 3, align_bytes=64)
+            run = 2 if engine == "gpsimd" else 4
+            dst = y_in[b, g, hf][:, first:last, :].rearrange("p (c i) t -> p c t i", i=run)
+            src = y_turned[b, g][:, :, hf * HALF + first : hf * HALF + last].rearrange("p t (c i) -> p c t i", i=run)
             if engine == "vector":
                 nc.vector.tensor_copy(out=dst, in_=src)
-            else:
+            elif engine == "scalar":
                 nc.scalar.copy(out=dst, in_=src)
+            else:
+                nc.gpsimd.tensor_scalar(out=dst, in0=src, scalar1=1.0, scalar2=0.0, op0=ALU.mult, op1=ALU.add)
 
-        def quantise_y(b, g, first=0, count=S):
-            codes = work.tile([P, count], U32, tag="yc", name="yc", bufs=3, align_bytes=64)
-            src = y_in[b, g][:, first : first + count, :].rearrange("p j t -> p (j t)")
-            cols = slice(b * S + first, b * S + first + count)
-            quantise(src, codes[:], y_scales[:, g, cols])
-            dst = out_1[g, :, cols, :].rearrange("p m t -> p (m t)")
-            nc.sync.dma_start(out=dst.bitcast(I32), in_=codes[:].bitcast(I32))
+        y_codes = {}
+
+        def quantise_y(b, g, hf):
+            if hf == 0:
+                y_codes[b, g] = work.tile([P, S], U32, tag="yc", name="yc", bufs=3, align_bytes=64)
+            codes = y_codes[b, g]
+            first = b * S + hf * HALF
+            src = y_in[b, g, hf][:].rearrange("p j t -> p (j t)")
+            quantise(src, codes[:, hf * HALF : (hf + 1) * HALF], y_scales[:, g, first : first + HALF])
+            if hf == 1:
+                dst = out_1[g, :, b * S : (b + 1) * S, :].rearrange("p m t -> p (m t)")
+                nc.sync.dma_start(out=dst.bitcast(I32), in_=codes[:].bitcast(I32))
+                if g == 1:
+                    store_scales(b, 1)
 
         warm_up(26, warm_codes, warm_scales)
         interleave_w(0, 0, "vector")
@@ -349,102 +359,112 @@ def tile_slot_mixing_latent_dynamics_h3_kernel(
         quantise_z(0, 1)
 
         def z_place(j):
-            q = j - 2 if j < 6 else (j + 2) // 2
+            q = (j + 1) // 2
             return 1 + q // 4, (q // 2) % 2, q % 2
 
         def turns_z(j):
-            return 2 <= j < 6 or (j >= 6 and j % 2 == 0 and z_place(j)[0] < B)
+            return j >= -1 and j % 2 == 1 and z_place(j)[0] < B
+
+        def y_half(q):
+            return q // 4, (q // 2) % 2, q % 2
 
         tail = STEPS - 2 * PACK
-        for j in range(STEPS + 1):
+        for j in range(STEPS + 2):
+            if j % 2 == 0 and j >= 6:
+                stage_two(j - 5)
             if j < STEPS:
                 stage_one(j)
+            if j % 2 == 1 and j >= 5:
+                stage_two(j - 5)
             if j == 0:
+                turn_z(*z_place(-1))
+            if j == 2:
                 turn_v(0)
                 turn_v(1)
-            if 0 <= j - 3 < STEPS:
-                stage_two(j - 3)
-            if 0 <= j - 8 < tail:
-                turn_y(j - 8, range(PACK))
+            if 0 <= j - 9 < tail:
+                turn_y(j - 9, range(PACK))
             if turns_z(j):
                 turn_z(*z_place(j))
             if 0 <= j - 1 < STEPS:
                 activate(j - 1)
-            if 0 <= j - 9 < tail:
-                store_y(j - 9, "scalar", 2)
+            if 0 <= j - 10 < tail:
+                store_y(j - 10, "scalar", 2)
             if j == 0:
                 scale_z(0, 0, 1, range(PACK))
             if j == 1:
+                copy_z(*z_place(-1))
+            if j == 3:
                 copy_v(0)
                 copy_v(1)
-            if j == 2:
-                scale_z(0, 1, 1, range(2))
-            if turns_z(j - 1):
+            if 0 < j < 8 and turns_z(j - 1):
                 copy_z(*z_place(j - 1))
-                scale_z(*z_place(j - 1), range(PACK if j < 7 else 1))
-            elif j > 7 and turns_z(j - 2):
-                scale_z(*z_place(j - 2), range(1, PACK if j % 1000 != 0 else 2))
-            if 0 <= j - 8 < tail and j - 8 >= 20:
-                b, g, k = where(j - 8)
-                round_y(b, g, k, 1, "scalar")
+            if turns_z(j - 2):
+                scale_z(*z_place(j - 2), range(0, 2))
+            if turns_z(j - 3):
+                scale_z(*z_place(j - 3), range(2, PACK))
+            if j in [5, 7]:
+                n = [5, 7].index(j)
+                scale_z(0, 1, 1, range(2 * (n % 2), 2 * (n % 2) + 2))
+            if j % 2 == 0 and j >= 12:
+                round_y(*y_half((j - 10) // 2), 224 if j < 23 else 128, HALF, "scalar")
             pieces = [(0, PACK + 2 * j), (0, PACK + 2 * j + 1)] if j < 2 else [(1, j + 2)] if j < 6 else []
             for g, i in pieces:
                 interleave_w(g, i, "vector")
-            if 0 <= j - 2 < STEPS:
-                scale_a(j - 2)
-            if j == 2:
+            if j == 4:
                 quantise(v_in[:].bitcast(BF16), v_codes[:], v_scales[:])
-            if 0 <= j - 4 < STEPS:
-                residual(j - 4)
-            for g, i in pieces:
-                quantise_w(g, i)
-            if 0 <= j - 2 < STEPS:
+            if j % 2 == 1 and j >= 3:
+                scale_a(j - 3)
+                scale_a(j - 2)
+                if turns_z(j - 2) and z_place(j - 2)[2] == 1:
+                    quantise_z(*z_place(j - 2)[:2])
+                for g, i in pieces:
+                    quantise_w(g, i)
+                quantise_a(j - 3)
+                if j == 9:
+                    round_y(0, 0, 0, 0, HALF, "vector")
+                if j >= 11:
+                    quantise_y(*y_half((j - 11) // 2))
                 quantise_a(j - 2)
-            if j in (3, 4):
-                scale_z_vector(0, 1, 0, j - 3)
-            if j == 5 and 2 == 2:
-                scale_z_vector(0, 1, 1, 1)
-            if j > 7 and j % 1000 == 0 and turns_z(j - 2):
-                scale_z_vector(*z_place(j - 2), 1)
-            if j >= 12 and j % 4 == 0:
-                b, g, k = where(j - 12)
-                quantise_y(b, g)
-                if g == 1:
-                    store_scales(b, 1)
-            if 0 <= j - 8 < min(tail, 20):
-                b, g, k = where(j - 8)
-                round_y(b, g, k, 1, "vector")
-            if j > 7 and j % 4 == 2 and j // 8 + 1 < B:
-                quantise_z(j // 8 + 1, (j // 4) % 2)
-            if j in (5, 6):
-                quantise_z(1, j - 5)
+                if j >= 11:
+                    round_y(*y_half((j - 9) // 2), 0, 224 if j < 22 else 128 if j < STEPS else HALF, "gpsimd")
+            if j in [0, 4]:
+                n = [0, 4].index(j)
+                scale_z_vector(0, 1, n // 2, n % 2)
+            if j % 2 == 0 and j >= 6:
+                residual(j - 6)
+                residual(j - 5)
+                if j >= 8 and turns_z(j - 1):
+                    copy_z(*z_place(j - 1), "vector")
+            if j % 2 == 0 or j < 3:
+                for g, i in pieces:
+                    quantise_w(g, i)
 
         tags = ("zt", "zt", "yt", "yt")
+        stage_two(STEPS - 3)
         for jb in range(PACK):
             turn_y(tail + jb, range(PACK), tags[jb])
-        stage_two(STEPS - 2)
-        warm_up(6, warm_codes, warm_scales)
-        scale_a(STEPS - 1)
+        stage_two(STEPS - 2, "s1")
+        stage_two(STEPS - 1, "s1")
+        round_y(B - 1, 0, 1, 0, 96, "gpsimd")
+        residual(STEPS - 4)
         residual(STEPS - 3)
-        quantise_a(STEPS - 1)
-        stage_two(STEPS - 1)
-        store_y(tail, "scalar", 2)
-        store_y(tail + 1, "scalar", 2)
-        round_y(B - 1, 0, 0, 1, "scalar")
-        store_y(tail + 2, "scalar", 2)
-        store_y(tail + 3, "scalar", 2)
+        for jb in range(PACK):
+            store_y(tail + jb, "scalar", 2)
+        round_y(B - 1, 0, 1, 96, HALF, "scalar")
         residual(STEPS - 2)
-        round_y(B - 1, 0, 1, PACK - 1, "vector")
         residual(STEPS - 1)
-        quantise_y(B - 1, 0)
+        quantise_y(B - 1, 0, 0)
+        quantise_y(B - 1, 0, 1)
         for jb in range(PACK):
-            turn_y(tail + PACK + jb, range(PACK - 1), tags[jb])
-        for jb in range(PACK):
-            turn_y(tail + PACK + jb, range(PACK - 1, PACK), tags[jb])
-        round_y(B - 1, 1, 0, PACK, "vector")
+            turn_y(tail + PACK + jb, range(PACK - 2), tags[jb])
+        for t in range(PACK - 2, PACK):
+            for jb in range(PACK):
+                turn_y(tail + PACK + jb, range(t, t + 1), tags[jb])
+        round_y(B - 1, 1, 0, 0, HALF, "vector")
+        round_y(B - 1, 1, 1, 0, HALF, "vector")
         store_y(tail + PACK, "scalar", 2)
         store_y(tail + PACK + 1, "scalar", 2)
-        quantise_y(B - 1, 1)
+        quantise_y(B - 1, 1, 0)
         store_y(tail + PACK + 2, "scalar", 2)
         store_y(tail + PACK + 3, "scalar", 2)
-        store_scales(B - 1, 1)
+        quantise_y(B - 1, 1, 1)

@@ -19,8 +19,24 @@ P = 128
 PACK = 4
 GROUP = P * PACK
 GROUPS = D // GROUP
+WORDS = GROUP // 2
 HALF = S // 2
+WIDE = 2 * P
 STEPS = B * GROUPS * PACK
+TAIL = STEPS - 2 * PACK
+
+SILU_LAG = 1
+SCALE_LAG = 3
+TWO_LAG = 5
+RESIDUAL_LAG = 6
+TURN_LAG = 9
+STORE_LAG = 10
+PLANE_LAG = 11
+
+POOL_SLOTS_LONG = 208
+POOL_SLOTS_SHORT = 128
+
+WARM_START, WARM_W, WARM_Z = 14, 5, 4
 
 
 def tile_slot_mixing_latent_dynamics_h3_kernel(
@@ -70,31 +86,30 @@ def tile_slot_mixing_latent_dynamics_h3_kernel(
 
         ident = const.tile([P, P], F32)
         make_identity(nc, ident[:])
-        warm = const.tile([P, 1], F32)
-        nc.scalar.activation(out=warm[:], in_=ident[:, 0:1], func=ACT.Silu)
+        table_warm = const.tile([P, 1], F32)
+        nc.scalar.activation(out=table_warm[:], in_=ident[:, 0:1], func=ACT.Silu)
         keep_f = const.tile([P, GROUPS, PACK], F32)
-        scale_rep = const.tile([P, P, PACK], F32)
-
+        scale_rep = const.tile([P, WIDE, PACK], F32)
         y_scales = const.tile([P, GROUPS, B * S], U8, align_bytes=64)
 
         def quantise(src, codes, scales):
             nc.vector.quantize_mx(out=codes.bitcast(FP8X4), scales=scales, in_=src)
 
-        warm_in = const.tile([P, S], BF16, align_bytes=64)
-        warm_codes = const.tile([P, P], U32, align_bytes=64)
-        warm_scales = const.tile([P, P], U8, align_bytes=64)
-        nc.vector.memset(warm_in[:], 1.0)
-        quantise(warm_in[:], warm_codes[:], warm_scales[:])
+        ones = const.tile([P, PACK * WIDE], BF16, align_bytes=64)
+        ones_codes = const.tile([P, WIDE], U32, align_bytes=64)
+        ones_scales = const.tile([P, WIDE], U8, align_bytes=64)
+        nc.vector.memset(ones[:], 1.0)
+        quantise(ones[:], ones_codes[:], ones_scales[:])
 
-        def warm_up(passes, warm_codes, warm_scales, tag="s1"):
-            bank = psum.tile([P, P], F32, tag=tag, name="warm_bank")
+        def warm_up(passes, codes, scales):
+            bank = psum.tile([P, WIDE], F32, tag="h", name="warm_bank")
             for n in range(passes):
                 nc.tensor.matmul_mx(
                     out=bank[:],
-                    lhsT=warm_codes[:, 0:P].bitcast(FP8X4),
-                    lhsT_scale=warm_scales[:, 0:P],
-                    rhs=warm_codes[:].bitcast(FP8X4),
-                    rhs_scale=warm_scales[:],
+                    lhsT=codes[:, 0:P].bitcast(FP8X4),
+                    lhsT_scale=scales[:, 0:P],
+                    rhs=codes[:].bitcast(FP8X4),
+                    rhs_scale=scales[:],
                     start=True,
                     stop=True,
                 )
@@ -102,21 +117,20 @@ def tile_slot_mixing_latent_dynamics_h3_kernel(
         w_in = {}
         w_mx = {}
 
-        def interleave_w(g, i, engine):
+        def interleave_w(g, i, copy):
             h, t = i // PACK, i % PACK
-            grouped = work.tile([P, P, PACK], BF16, tag="w_in", name="w_in", bufs=8, align_bytes=64)
-            src = w_rows[g, h][:].rearrange("p j (m t) -> p t m j", t=PACK)[:, t, :, :]
-            if engine == "vector":
-                nc.vector.tensor_copy(out=grouped[:], in_=src)
-            else:
-                nc.scalar.copy(out=grouped[:], in_=src)
-            w_in[g, i] = grouped
+            if (g, i // 2) not in w_in:
+                w_in[g, i // 2] = work.tile(
+                    [P, 2, P, PACK], BF16, tag="w_in", name="w_in", bufs=4, align_bytes=64
+                )
+            src = w_rows[g, h][:].rearrange("p j (m t) -> p t m j", t=PACK)
+            copy(out=w_in[g, i // 2][:, i % 2, :, :], in_=src[:, t, :, :])
 
-        def quantise_w(g, i):
-            codes = const.tile([P, P], U32, name="wc_%d_%d" % (g, i), align_bytes=64)
-            scales = const.tile([P, P], U8, name="ws_%d_%d" % (g, i), align_bytes=64)
-            quantise(w_in[g, i][:].rearrange("p m j -> p (m j)"), codes[:], scales[:])
-            w_mx[g, i] = (codes, scales)
+        def quantise_w(g, pair):
+            codes = const.tile([P, WIDE], U32, name="wc_%d_%d" % (g, pair), align_bytes=64)
+            scales = const.tile([P, WIDE], U8, name="ws_%d_%d" % (g, pair), align_bytes=64)
+            quantise(w_in[g, pair][:].rearrange("p t m j -> p (t m j)"), codes[:], scales[:])
+            w_mx[g, pair] = (codes, scales)
 
         def turn_words(rows, first_block, g, tag):
             bank = psum.tile([P, 2, HALF], F32, tag=tag, name="turned")
@@ -125,7 +139,7 @@ def tile_slot_mixing_latent_dynamics_h3_kernel(
                 for u in range(2):
                     nc.tensor.transpose(
                         bank[:, u, tb * P : (tb + 1) * P],
-                        words[:, first_block + tb, 256 * g + u : 256 * (g + 1) : 2],
+                        words[:, first_block + tb, WORDS * g + u : WORDS * (g + 1) : 2],
                         ident[:],
                     )
             return bank
@@ -135,44 +149,46 @@ def tile_slot_mixing_latent_dynamics_h3_kernel(
         z_mx = {}
         kept = {}
 
-        def turn_z(b, g, hf, tag="zt"):
+        def turn_z(b, g, hf, tag="z"):
             z_bank[b, g, hf] = turn_words(z_rows[b, hf], 0, g, tag)
 
-        def copy_z(b, g, hf, engine="scalar"):
+        def copy_z(b, g, hf):
             if hf == 0:
                 z_in[b, g] = work.tile([P, S * 2], F32, tag="z_in", name="z_in", bufs=3, align_bytes=64)
             dst = z_in[b, g][:].rearrange("p (s m u) -> p s m u", s=PACK, u=2)
-            (nc.scalar.copy if engine == "scalar" else nc.vector.tensor_copy)(
-                out=dst[:, :, 64 * hf : 64 * (hf + 1), :],
+            nc.scalar.copy(
+                out=dst[:, :, hf * HALF // PACK : (hf + 1) * HALF // PACK, :],
                 in_=z_bank[b, g, hf][:].rearrange("p u (m s) -> p s m u", s=PACK),
             )
 
-        def scale_z(b, g, hf, slots):
+        def kept_tile(b, g):
             if (b, g) not in kept:
                 kept[b, g] = work.tile([P, PACK, S], F32, tag="kept", name="kept", bufs=5)
+            return kept[b, g]
+
+        def keep_z_scalar(b, g, hf, u):
             halves = z_bank[b, g, hf][:].bitcast(BF16)
-            for t in slots:
+            for e in range(2):
+                t = 2 * u + e
                 nc.scalar.activation(
-                    out=kept[b, g][:, t, hf * HALF : (hf + 1) * HALF],
-                    in_=halves[:, t // 2, t % 2 : 2 * HALF : 2],
+                    out=kept_tile(b, g)[:, t, hf * HALF : (hf + 1) * HALF],
+                    in_=halves[:, u, e : 2 * HALF : 2],
                     func=ACT.Copy,
                     scale=keep_f[:, g, t : t + 1],
                 )
 
-        def scale_z_vector(b, g, hf, u):
-            if (b, g) not in kept:
-                kept[b, g] = work.tile([P, PACK, S], F32, tag="kept", name="kept", bufs=5)
+        def keep_z_vector(b, g, hf, u):
             halves = z_bank[b, g, hf][:].bitcast(BF16)
             nc.vector.tensor_tensor(
-                out=kept[b, g][:, 2 * u : 2 * u + 2, hf * HALF : (hf + 1) * HALF],
+                out=kept_tile(b, g)[:, 2 * u : 2 * u + 2, hf * HALF : (hf + 1) * HALF],
                 in0=halves[:, u, :].rearrange("p (j e) -> p e j", e=2),
                 in1=keep_f[:, g, 2 * u : 2 * u + 2].unsqueeze(2).to_broadcast([P, 2, HALF]),
                 op=ALU.mult,
             )
 
         def quantise_z(b, g):
-            codes = work.tile([P, S], U32, tag="zc", name="zc", bufs=4, align_bytes=64)
-            scales = work.tile([P, S], U8, tag="zs", name="zs", bufs=4, align_bytes=64)
+            codes = work.tile([P, S], U32, tag="zc", name="zc", bufs=2 * GROUPS, align_bytes=64)
+            scales = work.tile([P, S], U8, tag="zs", name="zs", bufs=2 * GROUPS, align_bytes=64)
             quantise(z_in[b, g][:].bitcast(BF16), codes[:], scales[:])
             z_mx[b, g] = (codes, scales)
 
@@ -182,7 +198,7 @@ def tile_slot_mixing_latent_dynamics_h3_kernel(
         v_bank = {}
 
         def turn_v(hf):
-            v_bank[hf] = turn_words(v_rows, 2 * hf, 0, "s2")
+            v_bank[hf] = turn_words(v_rows, 2 * hf, 0, "u")
 
         def copy_v(hf):
             dst = v_in[:].rearrange("p (j u) -> p j u", u=2)
@@ -200,56 +216,59 @@ def tile_slot_mixing_latent_dynamics_h3_kernel(
         y_bank = {}
         y_rows = {}
         y_in = {}
+        y_codes = {}
 
         def where(i):
             return i // (GROUPS * PACK), (i // PACK) % GROUPS, i % PACK
 
         def stage_one(i):
-            b, h, t = where(i)
-            bank = psum.tile([P, PACK, P], F32, tag="s1", name="h_bank")
-            for s in range(PACK):
-                slots = slice(s * P, (s + 1) * P)
+            b, pair, u = i // (GROUPS * PACK), (i // 2) % PACK, i % 2
+            bank = psum.tile([P, 2, WIDE], F32, tag="h", name="h_bank")
+            for e in range(2):
+                slots = slice((2 * u + e) * P, (2 * u + e + 1) * P)
                 for g in range(GROUPS):
                     nc.tensor.matmul_mx(
-                        out=bank[:, s, :],
+                        out=bank[:, e, :],
                         lhsT=z_mx[b, g][0][:, slots].bitcast(FP8X4),
                         lhsT_scale=z_mx[b, g][1][:, slots],
-                        rhs=w_mx[g, h * PACK + t][0][:].bitcast(FP8X4),
-                        rhs_scale=w_mx[g, h * PACK + t][1][:],
+                        rhs=w_mx[g, pair][0][:].bitcast(FP8X4),
+                        rhs_scale=w_mx[g, pair][1][:],
                         start=(g == 0),
                         stop=(g == GROUPS - 1),
                     )
             h_bank[i] = bank
 
         def activate(i):
-            silu[i] = work.tile([P, P * PACK], F32, tag="silu", name="silu", bufs=3)
+            if i % 2 == 0:
+                silu[i // 2] = work.tile([P, 2, 2 * WIDE], F32, tag="silu", name="silu")
             nc.scalar.activation(
-                out=silu[i][:].rearrange("p (m s) -> p m s", s=PACK),
-                in_=h_bank[i][:].rearrange("p s m -> p m s"),
+                out=silu[i // 2][:, i % 2, :].rearrange("p (f e) -> p f e", e=2),
+                in_=h_bank[i][:].rearrange("p e f -> p f e"),
                 func=ACT.Silu,
             )
 
-        def scale_a(i):
-            a_in[i] = work.tile([P, P * PACK], BF16, tag="a_in", name="a_in", bufs=3, align_bytes=64)
+        def scale_a(n):
+            a_in[n] = work.tile([P, WIDE, 2, 2], BF16, tag="a_in", name="a_in", align_bytes=64)
             nc.vector.tensor_tensor(
-                out=a_in[i][:],
-                in0=silu[i][:],
-                in1=scale_rep[:].rearrange("p m s -> p (m s)"),
+                out=a_in[n][:],
+                in0=silu[n][:].rearrange("p u (f e) -> p f u e", e=2),
+                in1=scale_rep[:].rearrange("p f (u e) -> p f u e", e=2),
                 op=ALU.mult,
             )
 
-        def quantise_a(i):
-            codes = work.tile([P, P], U32, tag="ac", name="ac", bufs=3, align_bytes=64)
-            scales = work.tile([P, P], U8, tag="as", name="as", bufs=3, align_bytes=64)
-            quantise(a_in[i][:], codes[:], scales[:])
-            a_mx[i] = (codes, scales)
+        def quantise_a(n):
+            codes = work.tile([P, WIDE], U32, tag="ac", name="ac", bufs=3, align_bytes=64)
+            scales = work.tile([P, WIDE], U8, tag="as", name="as", bufs=3, align_bytes=64)
+            quantise(a_in[n][:].rearrange("p f u e -> p (f u e)"), codes[:], scales[:])
+            a_mx[n] = (codes, scales)
 
-        def stage_two(i, tag="s2"):
+        def stage_two(i, tag="u"):
             bank = psum.tile([P, S], F32, tag=tag, name="u_bank")
+            cols = slice((i % 2) * P, (i % 2 + 1) * P)
             nc.tensor.matmul_mx(
                 out=bank[:],
-                lhsT=a_mx[i][0][:].bitcast(FP8X4),
-                lhsT_scale=a_mx[i][1][:],
+                lhsT=a_mx[i // 2][0][:, cols].bitcast(FP8X4),
+                lhsT_scale=a_mx[i // 2][1][:, cols],
                 rhs=v_codes[:].bitcast(FP8X4),
                 rhs_scale=v_scales[:],
                 start=True,
@@ -260,7 +279,7 @@ def tile_slot_mixing_latent_dynamics_h3_kernel(
         def residual(i):
             b, g, t = where(i)
             if t == 0:
-                y_turned[b, g] = work.tile([P, PACK, S], F32, tag="yt", name="y_turned", bufs=3)
+                y_turned[b, g] = work.tile([P, PACK, S], F32, tag="y_turned", name="y_turned", bufs=3)
             nc.vector.scalar_tensor_tensor(
                 out=y_turned[b, g][:, t, :],
                 in0=u_bank[i][:],
@@ -270,51 +289,44 @@ def tile_slot_mixing_latent_dynamics_h3_kernel(
                 op1=ALU.add,
             )
 
-        def turn_y(i, slots, tag="yt"):
+        def turn_y(i, slices, tag="y"):
             b, g, jb = where(i)
             if i not in y_bank:
                 y_bank[i] = psum.tile([P, PACK, P], F32, tag=tag, name="y_bank")
-            for t in slots:
+            for t in slices:
                 nc.tensor.transpose(y_bank[i][:, t, :], y_turned[b, g][:, t, jb * P : (jb + 1) * P], ident[:])
 
-        def store_y(i, engine, group):
+        def store_y(i):
             b, g, jb = where(i)
-            if jb % group == 0:
-                y_rows[b, g] = work.tile([P, group, GROUP], F32, tag="y_rows", name="y_rows", bufs=6)
+            if jb % 2 == 0:
+                y_rows[b, g] = work.tile([P, 2, GROUP], F32, tag="y_rows", name="y_rows", bufs=6)
             rows = y_rows[b, g]
-            dst = rows[:, jb % group, :].rearrange("p (m t) -> p m t", t=PACK)
-            src = y_bank[i][:].rearrange("p t m -> p m t")
-            if engine == "vector":
-                nc.vector.tensor_copy(out=dst, in_=src)
-            else:
-                nc.scalar.copy(out=dst, in_=src)
-            if jb % group == group - 1:
-                hbm = out_0[b, (jb + 1 - group) * P : (jb + 1) * P, g * GROUP : (g + 1) * GROUP]
-                nc.sync.dma_start(out=hbm.rearrange("(jb p) f -> p jb f", p=P), in_=rows[:])
+            nc.scalar.copy(
+                out=rows[:, jb % 2, :].rearrange("p (m t) -> p m t", t=PACK),
+                in_=y_bank[i][:].rearrange("p t m -> p m t"),
+            )
+            if jb % 2 == 1:
+                dst = out_0[b, (jb - 1) * P : (jb + 1) * P, g * GROUP : (g + 1) * GROUP]
+                nc.sync.dma_start(out=dst.rearrange("(jb p) f -> p jb f", p=P), in_=rows[:])
 
-        def store_scales(first, count):
-            cols = slice(first * S // 4, (first + count) * S // 4)
-            for q in range(4):
-                nc.sync.dma_start(
-                    out=out_2.bitcast(I32)[:, 4 * q : 4 * q + 4, cols].rearrange("g r m -> r g m"),
-                    in_=y_scales[32 * q : 32 * q + 4].bitcast(I32)[:, :, cols],
-                )
+        def copy_gpsimd(out, in_):
+            nc.gpsimd.tensor_scalar(out=out, in0=in_, scalar1=1.0, scalar2=0.0, op0=ALU.mult, op1=ALU.add)
 
-        def round_y(b, g, hf, first, last, engine):
+        def round_y(b, g, hf, first, last, copy, run=4):
             if (b, g, hf) not in y_in:
-                tag = "y_last" if (b, g, hf) > (B - 1, 0, 0) else "y_in"
-                y_in[b, g, hf] = work.tile([P, HALF, PACK], BF16, tag=tag, name=tag, bufs=1 if tag == "y_in" else 3, align_bytes=64)
-            run = 2 if engine == "gpsimd" else 4
-            dst = y_in[b, g, hf][:, first:last, :].rearrange("p (c i) t -> p c t i", i=run)
-            src = y_turned[b, g][:, :, hf * HALF + first : hf * HALF + last].rearrange("p t (c i) -> p c t i", i=run)
-            if engine == "vector":
-                nc.vector.tensor_copy(out=dst, in_=src)
-            elif engine == "scalar":
-                nc.scalar.copy(out=dst, in_=src)
-            else:
-                nc.gpsimd.tensor_scalar(out=dst, in0=src, scalar1=1.0, scalar2=0.0, op0=ALU.mult, op1=ALU.add)
+                own = (b, g, hf) > (B - 1, 0, 0)
+                y_in[b, g, hf] = work.tile(
+                    [P, HALF, PACK], BF16, tag="y_own" if own else "y_in", name="y_in",
+                    bufs=3 if own else 1, align_bytes=64,
+                )
+            slots = slice(hf * HALF + first, hf * HALF + last)
+            copy(
+                out=y_in[b, g, hf][:, first:last, :].rearrange("p (c i) t -> p c t i", i=run),
+                in_=y_turned[b, g][:, :, slots].rearrange("p t (c i) -> p c t i", i=run),
+            )
 
-        y_codes = {}
+        def round_y_gpsimd(b, g, hf, last):
+            round_y(b, g, hf, 0, last, copy_gpsimd, run=2)
 
         def quantise_y(b, g, hf):
             if hf == 0:
@@ -326,145 +338,143 @@ def tile_slot_mixing_latent_dynamics_h3_kernel(
             if hf == 1:
                 dst = out_1[g, :, b * S : (b + 1) * S, :].rearrange("p m t -> p (m t)")
                 nc.sync.dma_start(out=dst.bitcast(I32), in_=codes[:].bitcast(I32))
-                if g == 1:
-                    store_scales(b, 1)
+            if hf == 1 and g == GROUPS - 1:
+                cols = slice(b * S // 4, (b + 1) * S // 4)
+                for q in range(4):
+                    nc.sync.dma_start(
+                        out=out_2.bitcast(I32)[:, 4 * q : 4 * q + 4, cols].rearrange("g r m -> r g m"),
+                        in_=y_scales[32 * q : 32 * q + 4].bitcast(I32)[:, :, cols],
+                    )
 
-        warm_up(26, warm_codes, warm_scales)
-        interleave_w(0, 0, "vector")
-        interleave_w(0, 1, "vector")
+        warm_up(WARM_START, ones_codes, ones_scales)
+        interleave_w(0, 0, nc.vector.tensor_copy)
+        interleave_w(0, 1, nc.vector.tensor_copy)
+        interleave_w(0, 3, nc.scalar.copy)
+        interleave_w(0, 2, nc.vector.tensor_copy)
         quantise_w(0, 0)
-        warm_up(16, *w_mx[0, 0])
-        turn_z(0, 0, 0)
-        turn_z(0, 1, 0, "yt")
-        turn_z(0, 0, 1)
-        turn_z(0, 1, 1, "yt")
-        interleave_w(0, 2, "vector")
-        interleave_w(0, 3, "scalar")
+        warm_up(WARM_W, *w_mx[0, 0])
+        for hf in range(2):
+            turn_z(0, 0, hf)
+            turn_z(0, 1, hf, "y")
         nc.scalar.copy(out=keep_f[:], in_=keep_bf[:])
         for t in range(PACK):
-            interleave_w(1, t, "vector" if t < 2 else "scalar")
-        nc.scalar.copy(out=scale_rep[:], in_=scale_bf[:].unsqueeze(1).to_broadcast([P, P, PACK]))
-        for g in range(GROUPS):
-            for t in range(PACK):
-                if (g, t) != (0, 0):
-                    quantise_w(g, t)
-        warm_up(8, *w_mx[1, 3])
-        copy_z(0, 0, 0)
-        copy_z(0, 1, 0)
-        scale_z_vector(0, 0, 0, 0)
-        copy_z(0, 0, 1)
-        copy_z(0, 1, 1)
-        scale_z_vector(0, 0, 0, 1)
+            interleave_w(1, t, nc.vector.tensor_copy if t < 2 else nc.scalar.copy)
+        nc.scalar.copy(out=scale_rep[:], in_=scale_bf[:].unsqueeze(1).to_broadcast([P, WIDE, PACK]))
+        quantise_w(0, 1)
+        quantise_w(1, 0)
+        quantise_w(1, 1)
+        warm_up(WARM_Z, *w_mx[1, 1])
+        for hf in range(2):
+            copy_z(0, 0, hf)
+            copy_z(0, 1, hf)
+            keep_z_vector(0, 0, 0, hf)
         quantise_z(0, 0)
         quantise_z(0, 1)
 
-        def z_place(j):
-            q = (j + 1) // 2
-            return 1 + q // 4, (q // 2) % 2, q % 2
+        def half_group(n):
+            return n // (2 * GROUPS), (n // 2) % GROUPS, n % 2
+
+        def z_of(j):
+            return half_group(2 * GROUPS + (j + 1) // 2)
 
         def turns_z(j):
-            return j >= -1 and j % 2 == 1 and z_place(j)[0] < B
+            return j >= -1 and j % 2 == 1 and z_of(j)[0] < B
 
-        def y_half(q):
-            return q // 4, (q // 2) % 2, q % 2
-
-        tail = STEPS - 2 * PACK
         for j in range(STEPS + 2):
-            if j % 2 == 0 and j >= 6:
-                stage_two(j - 5)
+            odd = j % 2 == 1
+
+            if not odd and j > TWO_LAG:
+                stage_two(j - TWO_LAG)
             if j < STEPS:
                 stage_one(j)
-            if j % 2 == 1 and j >= 5:
-                stage_two(j - 5)
+            if odd and j >= TWO_LAG:
+                stage_two(j - TWO_LAG)
             if j == 0:
-                turn_z(*z_place(-1))
+                turn_z(*z_of(-1))
             if j == 2:
                 turn_v(0)
                 turn_v(1)
-            if 0 <= j - 9 < tail:
-                turn_y(j - 9, range(PACK))
+            if 0 <= j - TURN_LAG < TAIL:
+                turn_y(j - TURN_LAG, range(PACK))
             if turns_z(j):
-                turn_z(*z_place(j))
-            if 0 <= j - 1 < STEPS:
-                activate(j - 1)
-            if 0 <= j - 10 < tail:
-                store_y(j - 10, "scalar", 2)
+                turn_z(*z_of(j))
+
+            if 0 <= j - SILU_LAG < STEPS:
+                activate(j - SILU_LAG)
+            if 0 <= j - STORE_LAG < TAIL:
+                store_y(j - STORE_LAG)
             if j == 0:
-                scale_z(0, 0, 1, range(PACK))
+                keep_z_scalar(0, 0, 1, 0)
+                keep_z_scalar(0, 0, 1, 1)
             if j == 1:
-                copy_z(*z_place(-1))
+                copy_z(*z_of(-1))
             if j == 3:
                 copy_v(0)
                 copy_v(1)
-            if 0 < j < 8 and turns_z(j - 1):
-                copy_z(*z_place(j - 1))
+            if j > 0 and turns_z(j - 1):
+                copy_z(*z_of(j - 1))
             if turns_z(j - 2):
-                scale_z(*z_place(j - 2), range(0, 2))
-            if turns_z(j - 3):
-                scale_z(*z_place(j - 3), range(2, PACK))
-            if j in [5, 7]:
-                n = [5, 7].index(j)
-                scale_z(0, 1, 1, range(2 * (n % 2), 2 * (n % 2) + 2))
-            if j % 2 == 0 and j >= 12:
-                round_y(*y_half((j - 10) // 2), 224 if j < 23 else 128, HALF, "scalar")
-            pieces = [(0, PACK + 2 * j), (0, PACK + 2 * j + 1)] if j < 2 else [(1, j + 2)] if j < 6 else []
-            for g, i in pieces:
-                interleave_w(g, i, "vector")
-            if j == 4:
-                quantise(v_in[:].bitcast(BF16), v_codes[:], v_scales[:])
-            if j % 2 == 1 and j >= 3:
-                scale_a(j - 3)
-                scale_a(j - 2)
-                if turns_z(j - 2) and z_place(j - 2)[2] == 1:
-                    quantise_z(*z_place(j - 2)[:2])
-                for g, i in pieces:
-                    quantise_w(g, i)
-                quantise_a(j - 3)
-                if j == 9:
-                    round_y(0, 0, 0, 0, HALF, "vector")
-                if j >= 11:
-                    quantise_y(*y_half((j - 11) // 2))
-                quantise_a(j - 2)
-                if j >= 11:
-                    round_y(*y_half((j - 9) // 2), 0, 224 if j < 22 else 128 if j < STEPS else HALF, "gpsimd")
-            if j in [0, 4]:
-                n = [0, 4].index(j)
-                scale_z_vector(0, 1, n // 2, n % 2)
-            if j % 2 == 0 and j >= 6:
-                residual(j - 6)
-                residual(j - 5)
-                if j >= 8 and turns_z(j - 1):
-                    copy_z(*z_place(j - 1), "vector")
-            if j % 2 == 0 or j < 3:
-                for g, i in pieces:
-                    quantise_w(g, i)
+                keep_z_scalar(*z_of(j - 2), 0)
+            if j < PLANE_LAG and turns_z(j - 3):
+                keep_z_scalar(*z_of(j - 3), 1)
+            if j in (TURN_LAG - 4, TURN_LAG - 2):
+                keep_z_scalar(0, 1, 1, (j - TURN_LAG + 4) // 2)
+            if not odd and j > PLANE_LAG:
+                first = POOL_SLOTS_LONG if turns_z(j - 3) else POOL_SLOTS_SHORT
+                round_y(*half_group((j - STORE_LAG) // 2), first, HALF, nc.scalar.copy)
 
-        tags = ("zt", "zt", "yt", "yt")
+            if j < PACK:
+                interleave_w(j // 2, PACK + 2 * (j % 2), nc.vector.tensor_copy)
+                interleave_w(j // 2, PACK + 2 * (j % 2) + 1, nc.vector.tensor_copy)
+            if 1 <= j <= PACK:
+                quantise_w((j - 1) // 2, 2 + (j - 1) % 2)
+            if j == TWO_LAG - 1:
+                quantise(v_in[:].bitcast(BF16), v_codes[:], v_scales[:])
+            if odd and j >= SCALE_LAG:
+                scale_a((j - SCALE_LAG) // 2)
+                if turns_z(j - 2) and z_of(j - 2)[2] == 1:
+                    quantise_z(*z_of(j - 2)[:2])
+                if j == TURN_LAG:
+                    round_y(0, 0, 0, 0, HALF, nc.vector.tensor_copy)
+                if j >= PLANE_LAG:
+                    quantise_y(*half_group((j - PLANE_LAG) // 2))
+                quantise_a((j - SCALE_LAG) // 2)
+                if PLANE_LAG <= j < STEPS:
+                    last = POOL_SLOTS_LONG if turns_z(j - 2) else POOL_SLOTS_SHORT
+                    round_y_gpsimd(*half_group((j - TURN_LAG) // 2), last)
+            if j in (0, PACK):
+                keep_z_vector(0, 1, 0, j // PACK)
+            if not odd and j >= RESIDUAL_LAG:
+                residual(j - RESIDUAL_LAG)
+                residual(j - RESIDUAL_LAG + 1)
+                if j > PLANE_LAG and turns_z(j - 3):
+                    keep_z_vector(*z_of(j - 3), 1)
+
+        tags = ("z", "z", "y", "y")
+        round_y_gpsimd(B - 1, 0, 0, HALF)
         stage_two(STEPS - 3)
         for jb in range(PACK):
-            turn_y(tail + jb, range(PACK), tags[jb])
-        stage_two(STEPS - 2, "s1")
-        stage_two(STEPS - 1, "s1")
-        round_y(B - 1, 0, 1, 0, 96, "gpsimd")
+            turn_y(TAIL + jb, range(PACK), tags[jb])
+        stage_two(STEPS - 2, "h")
+        stage_two(STEPS - 1, "h")
+        round_y_gpsimd(B - 1, 0, 1, POOL_SLOTS_SHORT)
         residual(STEPS - 4)
         residual(STEPS - 3)
         for jb in range(PACK):
-            store_y(tail + jb, "scalar", 2)
-        round_y(B - 1, 0, 1, 96, HALF, "scalar")
+            store_y(TAIL + jb)
+        round_y(B - 1, 0, 1, POOL_SLOTS_SHORT, HALF, nc.scalar.copy)
         residual(STEPS - 2)
         residual(STEPS - 1)
         quantise_y(B - 1, 0, 0)
         quantise_y(B - 1, 0, 1)
         for jb in range(PACK):
-            turn_y(tail + PACK + jb, range(PACK - 2), tags[jb])
-        for t in range(PACK - 2, PACK):
+            turn_y(TAIL + PACK + jb, range(2), tags[jb])
+        for t in range(2, PACK):
             for jb in range(PACK):
-                turn_y(tail + PACK + jb, range(t, t + 1), tags[jb])
-        round_y(B - 1, 1, 0, 0, HALF, "vector")
-        round_y(B - 1, 1, 1, 0, HALF, "vector")
-        store_y(tail + PACK, "scalar", 2)
-        store_y(tail + PACK + 1, "scalar", 2)
-        quantise_y(B - 1, 1, 0)
-        store_y(tail + PACK + 2, "scalar", 2)
-        store_y(tail + PACK + 3, "scalar", 2)
-        quantise_y(B - 1, 1, 1)
+                turn_y(TAIL + PACK + jb, [t])
+        for hf in range(2):
+            round_y(B - 1, 1, hf, 0, HALF, nc.vector.tensor_copy)
+        for hf in range(2):
+            store_y(TAIL + PACK + 2 * hf)
+            store_y(TAIL + PACK + 2 * hf + 1)
+            quantise_y(B - 1, 1, hf)

@@ -36,9 +36,6 @@ PLANE_LAG = 11
 POOL_SLOTS_LONG = 208
 POOL_SLOTS_SHORT = 128
 
-WARM_START, WARM_W, WARM_Z = 14, 5, 4
-
-
 def tile_slot_mixing_latent_dynamics_h3_kernel(
     tc, latent, dyn_w, slot_scale, next_w, step, keep, out_0, out_1, out_2
 ):
@@ -86,33 +83,12 @@ def tile_slot_mixing_latent_dynamics_h3_kernel(
 
         ident = const.tile([P, P], F32)
         make_identity(nc, ident[:])
-        table_warm = const.tile([P, 1], F32)
-        nc.scalar.activation(out=table_warm[:], in_=ident[:, 0:1], func=ACT.Silu)
         keep_f = const.tile([P, GROUPS, PACK], F32)
         scale_rep = const.tile([P, WIDE, PACK], F32)
         y_scales = const.tile([P, GROUPS, B * S], U8, align_bytes=64)
 
         def quantise(src, codes, scales):
             nc.vector.quantize_mx(out=codes.bitcast(FP8X4), scales=scales, in_=src)
-
-        ones = const.tile([P, PACK * WIDE], BF16, align_bytes=64)
-        ones_codes = const.tile([P, WIDE], U32, align_bytes=64)
-        ones_scales = const.tile([P, WIDE], U8, align_bytes=64)
-        nc.vector.memset(ones[:], 1.0)
-        quantise(ones[:], ones_codes[:], ones_scales[:])
-
-        def warm_up(passes, codes, scales):
-            bank = psum.tile([P, WIDE], F32, tag="h", name="warm_bank")
-            for n in range(passes):
-                nc.tensor.matmul_mx(
-                    out=bank[:],
-                    lhsT=codes[:, 0:P].bitcast(FP8X4),
-                    lhsT_scale=scales[:, 0:P],
-                    rhs=codes[:].bitcast(FP8X4),
-                    rhs_scale=scales[:],
-                    start=True,
-                    stop=True,
-                )
 
         w_in = {}
         w_mx = {}
@@ -346,13 +322,11 @@ def tile_slot_mixing_latent_dynamics_h3_kernel(
                         in_=y_scales[32 * q : 32 * q + 4].bitcast(I32)[:, :, cols],
                     )
 
-        warm_up(WARM_START, ones_codes, ones_scales)
         interleave_w(0, 0, nc.vector.tensor_copy)
         interleave_w(0, 1, nc.vector.tensor_copy)
         interleave_w(0, 3, nc.scalar.copy)
         interleave_w(0, 2, nc.vector.tensor_copy)
         quantise_w(0, 0)
-        warm_up(WARM_W, *w_mx[0, 0])
         for hf in range(2):
             turn_z(0, 0, hf)
             turn_z(0, 1, hf, "y")
@@ -363,7 +337,6 @@ def tile_slot_mixing_latent_dynamics_h3_kernel(
         quantise_w(0, 1)
         quantise_w(1, 0)
         quantise_w(1, 1)
-        warm_up(WARM_Z, *w_mx[1, 1])
         for hf in range(2):
             copy_z(0, 0, hf)
             copy_z(0, 1, hf)

from contextlib import ExitStack

import concourse.mybir as mybir
from concourse.masks import make_identity

B, S, D = 4, 512, 1024
FLOPS = 2 * B * S * D * D + 2 * B * S * S * D

F32 = mybir.dt.float32
BF16 = mybir.dt.bfloat16
I32 = mybir.dt.int32
U32 = mybir.dt.uint32
U8 = mybir.dt.uint8
FP8X4 = mybir.dt.float8_e4m3fn_x4
ACT = mybir.ActivationFunctionType
ALU = mybir.AluOpType

P = 128
PACK = 4
GROUP = P * PACK
GROUPS = D // GROUP
WORDS = GROUP // 2
HALF = S // 2
WIDE = 2 * P
STEPS = B * GROUPS * PACK
TAIL = STEPS - 2 * PACK

SILU_LAG = 1
SCALE_LAG = 3
TWO_LAG = 5
RESIDUAL_LAG = 6
TURN_LAG = 9
STORE_LAG = 10
PLANE_LAG = 11

POOL_SLOTS_LONG = 208
POOL_SLOTS_SHORT = 128

def tile_slot_mixing_latent_dynamics_h3_kernel(
    tc, latent, dyn_w, slot_scale, next_w, step, keep, out_0, out_1, out_2
):
    nc = tc.nc
    with ExitStack() as ctx:
        const = ctx.enter_context(tc.tile_pool(name="const", bufs=1))
        work = ctx.enter_context(tc.tile_pool(name="work", bufs=2))
        psum = ctx.enter_context(tc.psum_pool(name="psum", bufs=2))
        ctx.enter_context(tc.manual_schedule())

        z_rows = {}
        w_rows = {}

        def load_z(b, hf):
            rows = const.tile([P, 2, D], BF16, name="z_%d_%d" % (b, hf))
            src = latent[b, hf * HALF : (hf + 1) * HALF, :]
            nc.sync.dma_start(out=rows[:], in_=src.rearrange("(tb p) d -> p tb d", p=P))
            z_rows[b, hf] = rows

        def load_w(g, h):
            rows = const.tile([P, PACK, GROUP], BF16, name="w_%d_%d" % (g, h))
            src = dyn_w[g * GROUP : (g + 1) * GROUP, h * GROUP : (h + 1) * GROUP]
            nc.sync.dma_start(out=rows[:], in_=src.rearrange("(p j) f -> p j f", j=PACK))
            w_rows[g, h] = rows

        keep_bf = const.tile([P, GROUPS, PACK], BF16)
        step_bf = const.tile([P, GROUPS, PACK], BF16)
        scale_bf = const.tile([P, PACK], BF16)
        v_rows = const.tile([P, PACK, S], BF16)
        load_w(0, 0)
        nc.scalar.dma_start(out=keep_bf[:], in_=keep.rearrange("(g p t) -> p g t", p=P, t=PACK))
        nc.scalar.dma_start(out=scale_bf[:], in_=slot_scale.rearrange("(p s) -> p s", s=PACK))
        load_w(1, 0)
        load_z(0, 0)
        load_z(0, 1)
        load_w(0, 1)
        load_z(1, 0)
        load_z(1, 1)
        nc.sync.dma_start(out=v_rows[:], in_=next_w.rearrange("(jb p) i -> p jb i", p=P))
        load_w(1, 1)
        nc.sync.dma_start(out=step_bf[:], in_=step.rearrange("(g p t) -> p g t", p=P, t=PACK))
        for b in range(2, B):
            load_z(b, 0)
            load_z(b, 1)

        ident = const.tile([P, P], F32)
        make_identity(nc, ident[:])
        keep_f = const.tile([P, GROUPS, PACK], F32)
        scale_rep = const.tile([P, WIDE, PACK], F32)
        y_scales = const.tile([P, GROUPS, B * S], U8, align_bytes=64)

        def quantise(src, codes, scales):
            nc.vector.quantize_mx(out=codes.bitcast(FP8X4), scales=scales, in_=src)

        w_in = {}
        w_mx = {}

        def interleave_w(g, i, copy):
            h, t = i // PACK, i % PACK
            if (g, i // 2) not in w_in:
                w_in[g, i // 2] = work.tile(
                    [P, 2, P, PACK], BF16, tag="w_in", name="w_in", bufs=4, align_bytes=64
                )
            src = w_rows[g, h][:].rearrange("p j (m t) -> p t m j", t=PACK)
            copy(out=w_in[g, i // 2][:, i % 2, :, :], in_=src[:, t, :, :])

        def quantise_w(g, pair):
            codes = const.tile([P, WIDE], U32, name="wc_%d_%d" % (g, pair), align_bytes=64)
            scales = const.tile([P, WIDE], U8, name="ws_%d_%d" % (g, pair), align_bytes=64)
            quantise(w_in[g, pair][:].rearrange("p t m j -> p (t m j)"), codes[:], scales[:])
            w_mx[g, pair] = (codes, scales)

        def turn_words(rows, first_block, g, tag):
            bank = psum.tile([P, 2, HALF], F32, tag=tag, name="turned")
            words = rows[:].bitcast(F32)
            for tb in range(2):
                for u in range(2):
                    nc.tensor.transpose(
                        bank[:, u, tb * P : (tb + 1) * P],
                        words[:, first_block + tb, WORDS * g + u : WORDS * (g + 1) : 2],
                        ident[:],
                    )
            return bank

        z_bank = {}
        z_in = {}
        z_mx = {}
        kept = {}

        def turn_z(b, g, hf, tag="z"):
            z_bank[b, g, hf] = turn_words(z_rows[b, hf], 0, g, tag)

        def copy_z(b, g, hf):
            if hf == 0:
                z_in[b, g] = work.tile([P, S * 2], F32, tag="z_in", name="z_in", bufs=3, align_bytes=64)
            dst = z_in[b, g][:].rearrange("p (s m u) -> p s m u", s=PACK, u=2)
            nc.scalar.copy(
                out=dst[:, :, hf * HALF // PACK : (hf + 1) * HALF // PACK, :],
                in_=z_bank[b, g, hf][:].rearrange("p u (m s) -> p s m u", s=PACK),
            )

        def kept_tile(b, g):
            if (b, g) not in kept:
                kept[b, g] = work.tile([P, PACK, S], F32, tag="kept", name="kept", bufs=5)
            return kept[b, g]

        def keep_z_scalar(b, g, hf, u):
            halves = z_bank[b, g, hf][:].bitcast(BF16)
            for e in range(2):
                t = 2 * u + e
                nc.scalar.activation(
                    out=kept_tile(b, g)[:, t, hf * HALF : (hf + 1) * HALF],
                    in_=halves[:, u, e : 2 * HALF : 2],
                    func=ACT.Copy,
                    scale=keep_f[:, g, t : t + 1],
                )

        def keep_z_vector(b, g, hf, u):
            halves = z_bank[b, g, hf][:].bitcast(BF16)
            nc.vector.tensor_tensor(
                out=kept_tile(b, g)[:, 2 * u : 2 * u + 2, hf * HALF : (hf + 1) * HALF],
                in0=halves[:, u, :].rearrange("p (j e) -> p e j", e=2),
                in1=keep_f[:, g, 2 * u : 2 * u + 2].unsqueeze(2).to_broadcast([P, 2, HALF]),
                op=ALU.mult,
            )

        def quantise_z(b, g):
            codes = work.tile([P, S], U32, tag="zc", name="zc", bufs=2 * GROUPS, align_bytes=64)
            scales = work.tile([P, S], U8, tag="zs", name="zs", bufs=2 * GROUPS, align_bytes=64)
            quantise(z_in[b, g][:].bitcast(BF16), codes[:], scales[:])
            z_mx[b, g] = (codes, scales)

        v_in = const.tile([P, S * 2], F32, align_bytes=64)
        v_codes = const.tile([P, S], U32, align_bytes=64)
        v_scales = const.tile([P, S], U8, align_bytes=64)
        v_bank = {}

        def turn_v(hf):
            v_bank[hf] = turn_words(v_rows, 2 * hf, 0, "u")

        def copy_v(hf):
            dst = v_in[:].rearrange("p (j u) -> p j u", u=2)
            nc.scalar.copy(
                out=dst[:, hf * HALF : (hf + 1) * HALF, :],
                in_=v_bank[hf][:].rearrange("p u j -> p j u"),
            )

        h_bank = {}
        silu = {}
        a_in = {}
        a_mx = {}
        u_bank = {}
        y_turned = {}
        y_bank = {}
        y_rows = {}
        y_in = {}
        y_codes = {}

        def where(i):
            return i // (GROUPS * PACK), (i // PACK) % GROUPS, i % PACK

        def stage_one(i):
            b, pair, u = i // (GROUPS * PACK), (i // 2) % PACK, i % 2
            bank = psum.tile([P, 2, WIDE], F32, tag="h", name="h_bank")
            for e in range(2):
                slots = slice((2 * u + e) * P, (2 * u + e + 1) * P)
                for g in range(GROUPS):
                    nc.tensor.matmul_mx(
                        out=bank[:, e, :],
                        lhsT=z_mx[b, g][0][:, slots].bitcast(FP8X4),
                        lhsT_scale=z_mx[b, g][1][:, slots],
                        rhs=w_mx[g, pair][0][:].bitcast(FP8X4),
                        rhs_scale=w_mx[g, pair][1][:],
                        start=(g == 0),
                        stop=(g == GROUPS - 1),
                    )
            h_bank[i] = bank

        def activate(i):
            if i % 2 == 0:
                silu[i // 2] = work.tile([P, 2, 2 * WIDE], F32, tag="silu", name="silu")
            nc.scalar.activation(
                out=silu[i // 2][:, i % 2, :].rearrange("p (f e) -> p f e", e=2),
                in_=h_bank[i][:].rearrange("p e f -> p f e"),
                func=ACT.Silu,
            )

        def scale_a(n):
            a_in[n] = work.tile([P, WIDE, 2, 2], BF16, tag="a_in", name="a_in", align_bytes=64)
            nc.vector.tensor_tensor(
                out=a_in[n][:],
                in0=silu[n][:].rearrange("p u (f e) -> p f u e", e=2),
                in1=scale_rep[:].rearrange("p f (u e) -> p f u e", e=2),
                op=ALU.mult,
            )

        def quantise_a(n):
            codes = work.tile([P, WIDE], U32, tag="ac", name="ac", bufs=3, align_bytes=64)
            scales = work.tile([P, WIDE], U8, tag="as", name="as", bufs=3, align_bytes=64)
            quantise(a_in[n][:].rearrange("p f u e -> p (f u e)"), codes[:], scales[:])
            a_mx[n] = (codes, scales)

        def stage_two(i, tag="u"):
            bank = psum.tile([P, S], F32, tag=tag, name="u_bank")
            cols = slice((i % 2) * P, (i % 2 + 1) * P)
            nc.tensor.matmul_mx(
                out=bank[:],
                lhsT=a_mx[i // 2][0][:, cols].bitcast(FP8X4),
                lhsT_scale=a_mx[i // 2][1][:, cols],
                rhs=v_codes[:].bitcast(FP8X4),
                rhs_scale=v_scales[:],
                start=True,
                stop=True,
            )
            u_bank[i] = bank

        def residual(i):
            b, g, t = where(i)
            if t == 0:
                y_turned[b, g] = work.tile([P, PACK, S], F32, tag="y_turned", name="y_turned", bufs=3)
            nc.vector.scalar_tensor_tensor(
                out=y_turned[b, g][:, t, :],
                in0=u_bank[i][:],
                scalar=step_bf[:, g, t : t + 1],
                in1=kept[b, g][:, t, :],
                op0=ALU.mult,
                op1=ALU.add,
            )

        def turn_y(i, slices, tag="y"):
            b, g, jb = where(i)
            if i not in y_bank:
                y_bank[i] = psum.tile([P, PACK, P], F32, tag=tag, name="y_bank")
            for t in slices:
                nc.tensor.transpose(y_bank[i][:, t, :], y_turned[b, g][:, t, jb * P : (jb + 1) * P], ident[:])

        def store_y(i):
            b, g, jb = where(i)
            if jb % 2 == 0:
                y_rows[b, g] = work.tile([P, 2, GROUP], F32, tag="y_rows", name="y_rows", bufs=6)
            rows = y_rows[b, g]
            nc.scalar.copy(
                out=rows[:, jb % 2, :].rearrange("p (m t) -> p m t", t=PACK),
                in_=y_bank[i][:].rearrange("p t m -> p m t"),
            )
            if jb % 2 == 1:
                dst = out_0[b, (jb - 1) * P : (jb + 1) * P, g * GROUP : (g + 1) * GROUP]
                nc.sync.dma_start(out=dst.rearrange("(jb p) f -> p jb f", p=P), in_=rows[:])

        def copy_gpsimd(out, in_):
            nc.gpsimd.tensor_scalar(out=out, in0=in_, scalar1=1.0, scalar2=0.0, op0=ALU.mult, op1=ALU.add)

        def round_y(b, g, hf, first, last, copy, run=4):
            if (b, g, hf) not in y_in:
                own = (b, g, hf) > (B - 1, 0, 0)
                y_in[b, g, hf] = work.tile(
                    [P, HALF, PACK], BF16, tag="y_own" if own else "y_in", name="y_in",
                    bufs=3 if own else 1, align_bytes=64,
                )
            slots = slice(hf * HALF + first, hf * HALF + last)
            copy(
                out=y_in[b, g, hf][:, first:last, :].rearrange("p (c i) t -> p c t i", i=run),
                in_=y_turned[b, g][:, :, slots].rearrange("p t (c i) -> p c t i", i=run),
            )

        def round_y_gpsimd(b, g, hf, last):
            round_y(b, g, hf, 0, last, copy_gpsimd, run=2)

        def quantise_y(b, g, hf):
            if hf == 0:
                y_codes[b, g] = work.tile([P, S], U32, tag="yc", name="yc", bufs=3, align_bytes=64)
            codes = y_codes[b, g]
            first = b * S + hf * HALF
            src = y_in[b, g, hf][:].rearrange("p j t -> p (j t)")
            quantise(src, codes[:, hf * HALF : (hf + 1) * HALF], y_scales[:, g, first : first + HALF])
            if hf == 1:
                dst = out_1[g, :, b * S : (b + 1) * S, :].rearrange("p m t -> p (m t)")
                nc.sync.dma_start(out=dst.bitcast(I32), in_=codes[:].bitcast(I32))
            if hf == 1 and g == GROUPS - 1:
                cols = slice(b * S // 4, (b + 1) * S // 4)
                for q in range(4):
                    nc.sync.dma_start(
                        out=out_2.bitcast(I32)[:, 4 * q : 4 * q + 4, cols].rearrange("g r m -> r g m"),
                        in_=y_scales[32 * q : 32 * q + 4].bitcast(I32)[:, :, cols],
                    )

        interleave_w(0, 0, nc.vector.tensor_copy)
        interleave_w(0, 1, nc.vector.tensor_copy)
        interleave_w(0, 3, nc.scalar.copy)
        interleave_w(0, 2, nc.vector.tensor_copy)
        quantise_w(0, 0)
        for hf in range(2):
            turn_z(0, 0, hf)
            turn_z(0, 1, hf, "y")
        nc.scalar.copy(out=keep_f[:], in_=keep_bf[:])
        for t in range(PACK):
            interleave_w(1, t, nc.vector.tensor_copy if t < 2 else nc.scalar.copy)
        nc.scalar.copy(out=scale_rep[:], in_=scale_bf[:].unsqueeze(1).to_broadcast([P, WIDE, PACK]))
        quantise_w(0, 1)
        quantise_w(1, 0)
        quantise_w(1, 1)
        for hf in range(2):
            copy_z(0, 0, hf)
            copy_z(0, 1, hf)
            keep_z_vector(0, 0, 0, hf)
        quantise_z(0, 0)
        quantise_z(0, 1)

        def half_group(n):
            return n // (2 * GROUPS), (n // 2) % GROUPS, n % 2

        def z_of(j):
            return half_group(2 * GROUPS + (j + 1) // 2)

        def turns_z(j):
            return j >= -1 and j % 2 == 1 and z_of(j)[0] < B

        for j in range(STEPS + 2):
            odd = j % 2 == 1

            if not odd and j > TWO_LAG:
                stage_two(j - TWO_LAG)
            if j < STEPS:
                stage_one(j)
            if odd and j >= TWO_LAG:
                stage_two(j - TWO_LAG)
            if j == 0:
                turn_z(*z_of(-1))
            if j == 2:
                turn_v(0)
                turn_v(1)
            if 0 <= j - TURN_LAG < TAIL:
                turn_y(j - TURN_LAG, range(PACK))
            if turns_z(j):
                turn_z(*z_of(j))

            if 0 <= j - SILU_LAG < STEPS:
                activate(j - SILU_LAG)
            if 0 <= j - STORE_LAG < TAIL:
                store_y(j - STORE_LAG)
            if j == 0:
                keep_z_scalar(0, 0, 1, 0)
                keep_z_scalar(0, 0, 1, 1)
            if j == 1:
                copy_z(*z_of(-1))
            if j == 3:
                copy_v(0)
                copy_v(1)
            if j > 0 and turns_z(j - 1):
                copy_z(*z_of(j - 1))
            if turns_z(j - 2):
                keep_z_scalar(*z_of(j - 2), 0)
            if j < PLANE_LAG and turns_z(j - 3):
                keep_z_scalar(*z_of(j - 3), 1)
            if j in (TURN_LAG - 4, TURN_LAG - 2):
                keep_z_scalar(0, 1, 1, (j - TURN_LAG + 4) // 2)
            if not odd and j > PLANE_LAG:
                first = POOL_SLOTS_LONG if turns_z(j - 3) else POOL_SLOTS_SHORT
                round_y(*half_group((j - STORE_LAG) // 2), first, HALF, nc.scalar.copy)

            if j < PACK:
                interleave_w(j // 2, PACK + 2 * (j % 2), nc.vector.tensor_copy)
                interleave_w(j // 2, PACK + 2 * (j % 2) + 1, nc.vector.tensor_copy)
            if 1 <= j <= PACK:
                quantise_w((j - 1) // 2, 2 + (j - 1) % 2)
            if j == TWO_LAG - 1:
                quantise(v_in[:].bitcast(BF16), v_codes[:], v_scales[:])
            if odd and j >= SCALE_LAG:
                scale_a((j - SCALE_LAG) // 2)
                if turns_z(j - 2) and z_of(j - 2)[2] == 1:
                    quantise_z(*z_of(j - 2)[:2])
                if j == TURN_LAG:
                    round_y(0, 0, 0, 0, HALF, nc.vector.tensor_copy)
                if j >= PLANE_LAG:
                    quantise_y(*half_group((j - PLANE_LAG) // 2))
                quantise_a((j - SCALE_LAG) // 2)
                if PLANE_LAG <= j < STEPS:
                    last = POOL_SLOTS_LONG if turns_z(j - 2) else POOL_SLOTS_SHORT
                    round_y_gpsimd(*half_group((j - TURN_LAG) // 2), last)
            if j in (0, PACK):
                keep_z_vector(0, 1, 0, j // PACK)
            if not odd and j >= RESIDUAL_LAG:
                residual(j - RESIDUAL_LAG)
                residual(j - RESIDUAL_LAG + 1)
                if j > PLANE_LAG and turns_z(j - 3):
                    keep_z_vector(*z_of(j - 3), 1)

        tags = ("z", "z", "y", "y")
        round_y_gpsimd(B - 1, 0, 0, HALF)
        stage_two(STEPS - 3)
        for jb in range(PACK):
            turn_y(TAIL + jb, range(PACK), tags[jb])
        stage_two(STEPS - 2, "h")
        stage_two(STEPS - 1, "h")
        round_y_gpsimd(B - 1, 0, 1, POOL_SLOTS_SHORT)
        residual(STEPS - 4)
        residual(STEPS - 3)
        for jb in range(PACK):
            store_y(TAIL + jb)
        round_y(B - 1, 0, 1, POOL_SLOTS_SHORT, HALF, nc.scalar.copy)
        residual(STEPS - 2)
        residual(STEPS - 1)
        quantise_y(B - 1, 0, 0)
        quantise_y(B - 1, 0, 1)
        for jb in range(PACK):
            turn_y(TAIL + PACK + jb, range(2), tags[jb])
        for t in range(2, PACK):
            for jb in range(PACK):
                turn_y(TAIL + PACK + jb, [t])
        for hf in range(2):
            round_y(B - 1, 1, hf, 0, HALF, nc.vector.tensor_copy)
        for hf in range(2):
            store_y(TAIL + PACK + 2 * hf)
            store_y(TAIL + PACK + 2 * hf + 1)
            quantise_y(B - 1, 1, hf)
